import numpy as np, ml_dtypes
CORES = [16,17,18,19,32,33,34,35]
N = 8
BF = ml_dtypes.bfloat16
def gentries(a):
    return np.ascontiguousarray(a.reshape(8, 16, -1).transpose(0, 2, 1)).reshape(8, -1)
def gtable(e):
    e = np.asarray(e); return np.ascontiguousarray(e.reshape(8, -1, 16).transpose(0, 2, 1)).reshape(128, -1).astype(np.int32)
S, LEN, RO = 512, 16, 4
W = N * S
FARTHEST = 2 ** 23
def parts(rng):
    own = S * np.arange(N)[:, None, None, None] + np.arange(S)[None, None, :, None]
    sc = np.exp2(3 + (np.log2(W) - 3.5) * rng.random((N, 8, 1, 16)))
    rf = (own + np.rint(sc * rng.standard_normal((N, 8, S, 16))).astype(np.int64)) % W
    hi = rng.integers(40, 256, (N, 8, 16, 1)); sz = 16 + (rng.random((N, 8, 16, S)) * (hi - 15)).astype(np.int64)
    lim = 135 * sc * np.where(sc > S // 2, 8, 1) * np.exp2(2 * rng.random((N, 8, 1, 16))) * (0.8 + 0.4 * rng.random((N, 8, 16, 16)))
    return np.minimum(sz, 255), rf, np.minimum(lim.astype(np.int64), FARTHEST)
def kinds(rng, fold, decoy, chain, strange):
    u = rng.random((N, 8, S)); k = np.where(u < fold, rng.integers(1, RO + 1, u.shape), 0); lo = fold
    for share, c in ((decoy, RO + 1), (chain, RO + 2), (strange, RO + 3)):
        k = np.where((u >= lo) & (u < lo + share), c, k); lo = lo + share
    k[..., S - RO:] = np.argsort(rng.random((N, 8, RO)), axis=-1) + 1; k[..., 0] = 0
    return k
def weave(rng, rf, kind, first=False):
    n = np.arange(S)
    def earlier(ok):
        order = np.argsort(~ok, axis=-1, kind="stable"); cnt = np.add.accumulate(ok.astype(np.int64), axis=-1) - ok
        j = np.minimum((rng.random(ok.shape) * cnt).astype(np.int64), np.maximum(cnt - 1, 0))
        return np.where(cnt > 0, np.take_along_axis(order, j, -1), n)
    def of(a, i): return np.take_along_axis(a, i[..., None], 2)
    rf = rf.copy(); m = (kind >= 1) & (kind <= RO); dec = kind == RO + 1
    root = np.zeros(kind.shape, np.int64) if first else earlier(kind == 0)
    cd = np.where(m | dec | (kind == RO + 3), root, n)
    cdw = (cd + S * np.arange(N)[:, None, None]).transpose(1, 0, 2).reshape(8, W)
    pos = np.ascontiguousarray(np.argsort(rng.random((N, 8, S, 16)), axis=-1)[..., :RO - 1]); x = np.zeros((N, 8, S, RO - 1), np.int64)
    for g in range(8):
        flat = kind[:, g].reshape(-1)
        for l in range(1, RO): x[:, g, :, l - 1] = rng.choice(np.flatnonzero(flat == l), (N, S))
    y = cdw[np.arange(8)[None, :, None, None], x]
    flip = rng.random(x.shape) < 0.4; x, y = np.where(flip, y, x), np.where(flip, x, y)
    np.put_along_axis(rf, pos, np.where((kind == 0)[..., None], y, np.take_along_axis(rf, pos, -1)), -1)
    base, bp, bx = of(rf, cd), of(pos, cd), of(x, cd)
    for l in range(1, RO):
        use = m & ((kind == l + 1) | ((kind > l + 1) & (rng.random(kind.shape) < 0.5))); p = bp[..., l - 1:l]
        np.put_along_axis(base, p, np.where(use[..., None], bx[..., l - 1:l], np.take_along_axis(base, p, -1)), -1)
    p = bp[..., :1]; v = np.take_along_axis(base, p, -1)
    np.put_along_axis(base, p, np.where(dec[..., None], (v // S + 1) % N * S, v), -1)
    rf = np.where((m | dec)[..., None], base, rf)
    c2 = earlier(m); ch = (kind == RO + 2) & (c2 != n)
    cd = np.where(ch, c2, cd); rl = of(rf, cd); pl = of(bp, cd)[..., :1]
    late = ch & (np.take_along_axis(kind, cd, -1) == 1) & (rng.random(kind.shape) < 0.6)
    np.put_along_axis(rl, pl, np.where(late[..., None], of(bx, cd)[..., :1], np.take_along_axis(rl, pl, -1)), -1)
    return np.where(ch[..., None], rl, rf), cd
def pack(sz, rf, cd, rch):
    return {"sz": np.ascontiguousarray(sz.reshape(N, 128, S)).astype(np.int32), "rf": np.ascontiguousarray(rf.transpose(0, 1, 3, 2)).reshape(N, 128, S).astype(np.int32),
            "cd": np.stack([gtable(a) for a in cd]), "rch": np.ascontiguousarray(rch.reshape(N, 128, 16)).astype(np.int32)}
def half():
    return (np.arange(N)[:, None] + np.arange(8)[None, :]) % 2 == 0
def setup_inputs(rng):
    sz, rf, rch = parts(rng); rf, cd = weave(rng, rf, kinds(rng, 0.24, 0.06, 0.06, 0.04))
    return pack(sz, rf, cd, rch)
def setup_inputs_spread(rng):
    sz, rf, rch = parts(rng)
    sz = 16 + (240 * np.power(rng.random((N, 8, 16, S)), np.exp2(rng.integers(-2, 4, (N, 8, 1, S))))).astype(np.int64)
    rch = np.exp2(4 + 18 * rng.random((N, 8, 1, 16)) + 3 * rng.random((N, 8, 16, 16))).astype(np.int64)
    rf, cd = weave(rng, rf, kinds(rng, 0.2, 0.08, 0.08, 0.08))
    return pack(np.minimum(sz, 255), rf, cd, np.minimum(rch, FARTHEST))
def setup_inputs_ends(rng):
    sz = np.where(rng.random((N, 8, 16, S)) < 0.5, 16, 255); sz[:, :, [1, 15]] = 255; sz[:, :, [0, 14]] = 16
    k = kinds(rng, 0.05, 0.08, 0.0, 0.55); k[:, 1::2, S - 1] = 0
    for g in range(0, 8, 2): k[N - 1, g, S - 1] = 1 + (g >> 1) % (RO - 1)
    m = 2 ** 20 // (S * (252 + 9 * LEN))
    many = (2 ** 20 / (S * m * (1 - np.mean(k == 1))) - 255) / LEN
    few = np.floor(many * np.arange(8 * N + 1)).astype(np.int64); few = 16 - (few[1:] - few[:-1]).reshape(N, 8, 1, 1)
    o = rng.random((N, 8, 1, 16)); o[..., 0] = -1; o[..., 15] = 2; o[:N - m, ::2, :, 15] = -1
    late = np.argsort(np.argsort(o, axis=-1), axis=-1) < few
    zero = rng.random((N, 8, 16, 16)) < 0.5; zero[:, :, np.arange(16), np.arange(16)] = True
    rch = np.where(late | ~zero, FARTHEST, 0)
    away = np.where(2 * np.arange(N) < N, W - 1, 0)[:, None, None, None]
    rf = np.where(rng.random((N, 8, S, 16)) < 0.5, 0, W - 1); rf = np.where(late & (rng.random(rf.shape) < 0.8), away, rf)
    rf, cd = weave(rng, rf, k, True)
    n = np.arange(S); own = S * np.arange(N)[:, None, None] + n
    fold = (cd != n) & np.all(rf == np.take_along_axis(rf, cd[..., None], 2), axis=-1)
    cnt = np.add.reduce(((rf != own[..., None]) & ~late).astype(np.int64), axis=-1)
    ln = np.where(fold, 0, 255 + LEN * cnt).reshape(-1); at = np.add.accumulate(ln) - ln
    gone = fold.reshape(-1).copy(); free = (((k == 0) | (k > RO)) & ~fold).reshape(-1); less = 0; last = 0
    for q in range(N - m):
        for g in range(8):
            ks = np.flatnonzero(late[q, g, 0]); ws = rng.permutation(1 + np.flatnonzero(k[q, g, 1:S // 4] == RO + 3))
            for i in range(2):
                vs = rng.permutation(np.arange((1 + i) * S // 4, (2 + i) * S // 4 - 12)); vs = vs[k[q, g, vs] == RO + 3]
                if i == 0: vs = vs[at[(q * 8 + g) * S + vs] % 2 == 1]
                if len(vs) == 0 or len(ws) < 2: continue
                v, w = int(vs[0]), int(ws[i])
                want = int(at[(q * 8 + g) * S + v]) + FARTHEST + i * int(rng.integers(0, 2)) + less
                u = int(np.searchsorted(at, want)); b = u % S
                if u // S != (q + m) * 8 + g or b < 8 or b >= S - 8 or u - 8 < last: continue
                cuts = [j for j in range(u - 1, u - 7, -1) if not gone[j]][:3]
                if len(cuts) < 3 or not (free[u] and free[u + 1]): continue
                rest = int(at[u]) - want; less += rest
                for j in cuts:
                    cut = min(rest, 239); rest -= cut
                    sz[j // (8 * S), j // S % 8, [1, 15], j % S] -= cut
                to = (q + m) * S + b
                if i == 0:
                    cd[q + m, g, b] = 0; cd[q + m, g, b + 1] = b; rf[q + m, g, [b, b + 1]] = rf[q + m, g, 0]
                    gone[u] = True; gone[u + 1] = True; less += int(ln[u] + ln[u + 1]); to += 1
                last = u + 1
                kk = int(ks[-1]) if i == 0 else int(rng.choice(ks)); p = int(rng.choice(np.flatnonzero(~late[q, g, 0])))
                x = int(rng.choice(np.flatnonzero(fold[:, g].reshape(-1)))); y = x // S * S + int(cd[x // S, g, x % S])
                rf[q, g, w] = rf[q, g, v]; rf[q, g, [w, v], kk] = to
                rf[q, g, w, p], rf[q, g, v, p] = (y, x) if rng.random() < 0.5 else (x, y)
                cd[q, g, v] = w
    return pack(sz, rf, cd, rch)
def setup_inputs_corners(rng):
    sz, rf, rch = parts(rng); k = kinds(rng, 0.24, 0.06, 0.1, 0.04); other = half(); k[other] = RO + 4
    rf, cd = weave(rng, rf, k); n = np.arange(S)
    for q, g in np.argwhere(other).tolist():
        t = (g // 2 + q) % 6; o = q * S; few = np.array([0, W - 1, o, o + S - 1, o + S // 2, (q + 1) % N * S + S - 1])
        if t < 3:
            rf[q, g] = rng.permutation(np.concatenate([few, rng.choice(few, 10)])); cd[q, g] = (np.maximum(n - 1, 0), 0 * n, n)[t]
        elif t == 3:
            rf[q, g] = (o + n)[:, None]; cd[q, g] = np.maximum(n - 1, 0)
        elif t == 4:
            cd[q, g] = np.minimum((rng.random(S) * (n + 1)).astype(np.int64), n); rch[q, g] = FARTHEST; sz[q, g] = 255
        else:
            j = rng.integers(0, 3, (S, 16)); rf[q, g] = np.where(j == 0, 0, np.where(j == 1, W - 1, (o + n)[:, None]))
            cd[q, g] = np.where(n % 2 == 1, 0, n); sz[q, g] = rng.choice(np.array([16, 255]), (16, S))
        if t in (2, 3, 5): rch[q, g] = 0
    return pack(sz, rf, cd, rch)
def setup_inputs_crowd(rng):
    sz, rf, rch = parts(rng); k = kinds(rng, 0.24, 0.06, 0.06, 0.04); other = half(); k[other] = RO + 4
    rf, cd = weave(rng, rf, k); n = np.arange(S)
    for q, g in np.argwhere(other).tolist():
        t = (g // 2 + q) % 4; pool = np.flatnonzero(k[:, g].reshape(-1) == 1 + (g // 2) % (RO - 1))
        rf[q, g] = int(rng.choice(pool)); rch[q, g] = 0; sz[q, g, ::2] = 255; sz[q, g, 1::4] = 16
        if t == 1: rf[q, g, :, int(rng.integers(0, 16))] = q * S + n
        if t == 2: cd[q, g] = np.minimum((rng.random(S) * n).astype(np.int64), np.maximum(n - 1, 0))
        if t == 3:
            rf[q, g] = rng.choice(pool, 4)[rng.integers(0, 4, 16)]; rf[q, g, S - 1, 15] = q * S + S - 1; cd[q, g] = 0
    return pack(sz, rf, cd, rch)
def setup_inputs_calm(rng):
    sz, rf, rch = parts(rng); k = kinds(rng, 0.24, 0.06, 0.06, 0.04); other = half(); k[other] = RO + 4
    rf, cd = weave(rng, rf, k); n = np.arange(S); m = S // 4 - 1
    for q, g in np.argwhere(other).tolist():
        o = q * S; dist = int(rng.integers(370, 401)); i = int(rng.integers(0, 16)); big = rng.random(m) < 0.4
        b = np.where(big, rng.integers(15, 17, m), rng.integers(0, 4, m)); c = np.where(big, rng.integers(15, 17, m), rng.integers(1, 4, m))
        e = (rng.random((3, m)) < np.array([[0.8], [0.75], [0.5]])).astype(np.int64)
        s1 = np.where(big, rng.integers(17, 35, m), rng.integers(150, 181, m))
        s0 = dist - LEN * b + e[0] - s1; s2 = dist - LEN * c + e[1] - s1; s3 = dist - LEN * c + e[2] - s2
        sz[q, g, i, :4 * m] = np.stack([s3, s2, s1, s0], axis=1).reshape(-1)
        rch[q, g] = FARTHEST; rch[q, g, i] = dist
        put = np.argsort(rng.random((m, 4, 16)), axis=-1) < np.stack([c, c, c, b], axis=1)[..., None]
        self_ = np.repeat((o + n)[:, None], 16, axis=1); to = self_[:4 * m].reshape(m, 4, 16) + 2
        to[:, 3] = (q + rng.integers(1, N, (m, 16))) % N * S + rng.integers(0, S, (m, 16))
        self_[:4 * m] = np.where(put, to, to * 0 + self_[:4 * m].reshape(m, 4, 16)).reshape(4 * m, 16)
        rf[q, g] = self_; cd[q, g] = np.minimum((rng.random(S) * (n + 1)).astype(np.int64), n)
    return pack(sz, rf, cd, rch)
def check_inputs(d):
    bad = []
    for k, lo, hi in (("sz", 16, 255), ("rf", 0, W - 1), ("cd", 0, S - 1), ("rch", 0, FARTHEST)):
        if np.min(d[k]) < lo or np.max(d[k]) > hi: bad.append("range of " + k)
    if any(np.any(gentries(a) > np.arange(S)) for a in d["cd"]): bad.append("cd names a later section")
    return bad
def places(z):
    t = np.ascontiguousarray(z.transpose(2, 0, 1, 3)).reshape(16, N * 8 * S)
    return np.ascontiguousarray((np.add.accumulate(t, axis=1) - t).reshape(16, N, 8, S).transpose(1, 2, 0, 3))
def reference(sz, rf, cd, rch):
    z = sz.astype(np.int64).reshape(N, 8, 16, S); lim = rch.astype(np.int64).reshape(N, 8, 16, 16)
    r = np.stack([gentries(a) for a in rf]).astype(np.int64).reshape(N, 8, S, 16); c = np.stack([gentries(a) for a in cd]).astype(np.int64)
    first = S * np.arange(N)[:, None, None]; n = np.arange(S)
    far = np.zeros((N, 8, S, 16), bool); gone = np.zeros((N, 8, S), bool); j = np.zeros((N, 8, S), np.int64) + first + n
    for rnd in range(RO):
        jw = j.transpose(1, 0, 2).reshape(8, W)
        r = jw[np.arange(8)[None, :, None, None], r]
        a = places(z); aw = np.ascontiguousarray(a.transpose(1, 2, 0, 3)).reshape(8, 16, W)
        now = np.zeros((N, 8, S, 16), bool)
        for q in range(N):
            for g in range(8):
                d = np.abs(aw[g][:, r[q, g]] - a[q, g][:, :, None])
                now[q, g] = np.any(d > lim[q, g][:, None, :], axis=0)
        new = now & ~far & ~gone[..., None]; far = far | new
        like = np.all(r == np.take_along_axis(r, c[..., None], 2), axis=-1)
        fold = ~gone & (c != n) & like
        grow = LEN * np.add.reduce(new.astype(np.int64), axis=-1)
        z = np.where(fold[:, :, None, :], 0, z + grow[:, :, None, :])
        gone = gone | fold; j = np.where(gone, first + c, first + n)
    return {"yr": np.ascontiguousarray(r.transpose(0, 1, 3, 2)).reshape(N, 128, S).astype(np.float32), "yj": j.astype(np.float32),
            "yf": np.ascontiguousarray(far.transpose(0, 1, 3, 2)).reshape(N, 128, S).astype(np.float32), "ya": places(z).reshape(N, 128, S).astype(np.float32)}

@@ -1,0 +1,507 @@
+from concourse.bass import DstId, RemoteDMATransfer
+from concourse.mybir import AluOpType as A, ActivationFunctionType as F, AxisListType as AX
+
+N, S, RO = 8, 512, 4
+MID = -131072.0
+
+PLAN = {"U": 0.56, "G": 0.89, "P": 0.27, "s": 0.1, "dma": 2.6, "msg": 5.0, "first": 8.0, "big": 9.0, "lag": 2, "hold": 0.7, "both": 13, "early": 3}
+
+f32, bf, h16, i32, u16 = "float32", "bfloat16", "float16", "int32", "uint16"
+
+
+def _sb(n, d):
+    return ("sbuf", [128, n], d)
+
+
+SCRATCH = {
+    "szi": _sb(512, i32), "rfi": _sb(512, i32), "szb": _sb(512, bf), "rfh": _sb(512, h16),
+    "ms": ("sbuf", [128, 128, 5], bf), "ls": ("sbuf", [128, 128, 5], bf), "mr": _sb(512, h16), "lr": _sb(512, h16),
+    "sc": ("dram", [8, 128, 4], i32), "dc": ("dram", [8, 128, 4], i32), "sh": ("dram", [8, 128, 2], i32), "dh": ("dram", [8, 128, 2], i32),
+    "cdi": _sb(32, i32), "rchi": _sb(16, i32), "cdu": _sb(32, u16), "rchf": _sb(16, f32), "nrch": _sb(16, f32),
+    "nn": _sb(512, bf), "zero": _sb(512, f32), "ai": _sb(4, i32), "col": _sb(16, f32),
+    "cb": _sb(128, f32), "cp": _sb(128, f32), "tmpc": _sb(128, f32),
+    "ib": _sb(128, bf), "ih": _sb(128, h16), "ni": _sb(128, bf), "ibig": _sb(128, bf), "nib": _sb(128, bf),
+    "blk512": _sb(128, bf), "blk16": _sb(128, bf), "ee": _sb(128, f32), "e2": _sb(128, f32),
+    "wd": _sb(144, bf), "we": _sb(1152, h16), "sel": _sb(1024, bf),
+    "eq": _sb(8, f32), "lt": _sb(8, f32), "uu": _sb(8, f32), "mc": _sb(8, f32), "mid8": _sb(8, f32),
+    "tot0": _sb(8, f32), "x8": _sb(8, f32), "z8": _sb(8, f32), "pre": _sb(16, f32), "bias": _sb(8, f32), "own": _sb(8, f32),
+    "tot": _sb(96, f32),
+    "szr": _sb(512, bf), "ll": _sb(520, f32), "l2": _sb(1024, f32), "ln": _sb(512, f32), "hi": _sb(512, bf), "lo": _sb(512, bf),
+    "lst": _sb(512, u16), "ml": _sb(96, u16), "bwin": _sb(4096, f32), "mwin": _sb(4096, bf),
+    "dd": _sb(8192, f32), "ind": _sb(8192, bf), "gr": _sb(8192, bf),
+    "rr": _sb(512, f32), "r2": _sb(512, f32), "neq": _sb(512, bf), "cc": _sb(512, bf), "jj": _sb(512, bf), "mm": _sb(512, bf),
+    "dead": _sb(512, bf), "far": _sb(512, bf),
+    "sr": ("dram", [8, 128, 64], f32), "dr": ("dram", [8, 128, 64], f32),
+    "sj": ("dram", [8, 128, 64], bf), "dj": ("dram", [8, 128, 64], bf),
+    "jn": _sb(512, bf), "j8": _sb(512, bf), "j8f": _sb(512, f32), "deadn": _sb(512, bf),
+    "ft": ("sbuf", [128, 128, 5], bf), "lf": ("sbuf", [128, 128, 5], bf),
+    "farn": _sb(512, bf), "yfb": _sb(512, f32), "lnn": _sb(512, f32), "la": _sb(520, f32),
+    "pf": ("psum", [128, 512], f32), "pr": ("psum", [128, 512], f32), "pm": ("psum", [128, 512], f32), "pn": ("psum", [128, 512], f32),
+    "pt0": ("psum", [128, 512], f32), "pt1": ("psum", [128, 512], f32), "pt2": ("psum", [128, 512], f32), "pt3": ("psum", [128, 512], f32),
+}
+_MSG = ["rc", "cd", "sz", "rf", "t1", "t2", "t3", "ro", "jo", "fo"]
+_DMA = ["lsz", "lrf", "sth", "stc", "stown", "lrc", "lcd", "mw1", "mw2", "mw3", "r1", "r2", "r3", "r4", "l1", "l2", "l3", "l4", "str", "rown", "stj", "jown", "yr", "ljn", "lj8", "yj", "yf", "ya"]
+SEMAPHORES = ["V", "S", "P", "G"] + ["a_" + m for m in _MSG] + ["o_" + m for m in _MSG] + ["d_" + d for d in _DMA]
+
+
+def engine_split(src, cores, topo):
+    others = [c for c in cores if c != src]
+    off = [c for c in others if topo.chip(c) != topo.chip(src)]
+    on = [c for c in others if topo.chip(c) == topo.chip(src)]
+    res = {}
+    used = []
+    for grp in (off, on):
+        if not grp:
+            continue
+        pool = [e for e in topo.engines(src, grp[0]) if e not in used]
+        each = 1
+        while each * 2 * len(grp) <= len(pool):
+            each *= 2
+        cnt = [each] * len(grp)
+        left = len(pool) - each * len(grp)
+        for q in range(len(grp)):
+            if left >= each:
+                cnt[q] += each
+                left -= each
+        at = 0
+        for c, n in zip(grp, cnt):
+            res[c] = pool[at:at + n]
+            at += n
+        used += pool[:at]
+    return res
+
+
+def place(calls):
+    n = len(calls)
+    end, queue, order = [None] * n, [None] * n, []
+    free = {q: 0.0 for q in "VSPGY-"}
+    users = [[] for _ in range(n)]
+    left = [len(c["deps"]) for c in calls]
+    for i, c in enumerate(calls):
+        for d in c["deps"]:
+            users[d].append(i)
+    cand = set(i for i in range(n) if left[i] == 0)
+
+    def ready(i, q):
+        return max([end[d] + (0.0 if q == "P" and queue[d] == "P" or q == "-" else PLAN["s"]) for d in calls[i]["deps"]] + [0.0])
+
+    def soon(i, depth):
+        t = 0.0
+        for d in calls[i]["deps"]:
+            if end[d] is not None:
+                t = max(t, end[d] + PLAN["s"])
+            elif depth == 0:
+                return 1e9
+            else:
+                q, (_, c) = min(calls[d]["alts"].items())
+                t = max(t, max(soon(d, depth - 1), free[q] if q == "P" else 0.0) + c + calls[d]["lat"] + PLAN["s"])
+        return t
+
+    while cand:
+        best = None
+        for i in cand:
+            for q in calls[i]["alts"]:
+                key = (max(free[q], ready(i, q)) if q != "-" else ready(i, q), i, q)
+                if best is None or key < best:
+                    best = key
+        t, i, q = best
+        if q in "VS" and calls[i]["alts"][q][1] > 0.3:
+            wait = None
+            for j in range(max(0, i - 120), i):
+                if end[j] is None and calls[j]["hot"] and q in calls[j]["alts"]:
+                    tj = soon(j, 3)
+                    if t < tj <= t + PLAN["hold"]:
+                        wait = tj if wait is None else min(wait, tj)
+            if wait is not None:
+                free[q] = wait + 1e-6
+                continue
+        cand.remove(i)
+        c = calls[i]["alts"][q][1]
+        if q != "-":
+            free[q] = t + c
+        end[i], queue[i] = t + c + calls[i]["lat"], q
+        order.append((i, q))
+        for u in users[i]:
+            left[u] -= 1
+            if left[u] == 0:
+                cand.add(u)
+    return order
+
+
+def rank_program(g, core, T, topo):
+    me = T.rank_of(core)
+    if me is None:
+        return
+    cores = list(T.cores)
+    Q = {"V": g.vector, "S": g.scalar, "P": g.tensor, "G": g, "Y": g.sync}
+    U, GU, PU, SM = PLAN["U"], PLAN["G"], PLAN["P"], PLAN["s"]
+    split = engine_split(core, cores, topo)
+    arrive = sum(len(engine_split(c, cores, topo)[core]) for c in cores if c != core)
+    nsent = sum(len(v) for v in split.values())
+
+    calls, writer, readers, hot = [], {}, {}, [False]
+
+    def op(alts, rd, wr, lat=0.0, tok=None, more=()):
+        deps = set(more)
+        for k in rd:
+            if k in writer:
+                deps.add(writer[k])
+        for k in wr:
+            if k in writer:
+                deps.add(writer[k])
+            deps.update(readers.get(k, []))
+        i = len(calls)
+        calls.append({"alts": alts, "deps": sorted(deps), "lat": lat, "tok": tok, "hot": hot[0]})
+        for k in rd:
+            readers.setdefault(k, []).append(i)
+        for k in wr:
+            writer[k] = i
+            readers[k] = []
+        return i
+
+    def dmas(q, name, pairs, rd, wr):
+        def emit():
+            for o, i in pairs:
+                Q[q].dma_start(o, i).then_inc(T.sem["d_" + name], 16)
+        op({q: (emit, 0.06 * len(pairs))}, rd, wr, PLAN["dma"], ("d_" + name, 16 * len(pairs)))
+
+    def send(name, src, dst, rd, land, lat):
+        tr = []
+        for r, c in enumerate(cores):
+            if c == core:
+                continue
+            rid, pid, _ = topo.addr(c)
+            m = 0
+            for e in split[c]:
+                m |= 1 << e
+            tr.append(RemoteDMATransfer(dst_ids=[DstId(rid=rid, pnc=pid)], dma_engine_mask=m, remote_sem=T.sem["a_" + name], src=src(r), dst=dst))
+        i = op({"G": (lambda: g.remote_dma_fused(tr, local_sem=T.sem["o_" + name]), 0.3)}, rd, ["sends"], 0.0, ("o_" + name, nsent))
+        op({"-": (None, 0.0)}, [], [land], lat, ("a_" + name, arrive), [i])
+
+    def f_ts(out, in0, s1, s2, o0, o1):
+        if o1 is None:
+            return lambda: g.vector.tensor_scalar(out, in0, s1, None, o0)
+        return lambda: g.vector.tensor_scalar(out, in0, s1, s2, o0, o1)
+
+    def f_act(out, a, fn, **kw):
+        return lambda: g.scalar.activation(out, a, fn, **kw)
+
+    def ts(out, in0, s1, s2, o0, o1, rd, wr, c=SM):
+        op({"V": (f_ts(out, in0, s1, s2, o0, o1), c)}, rd, wr)
+
+    def tt(out, a, b, o, rd, wr, c=SM):
+        op({"V": (lambda: g.vector.tensor_tensor(out, a, b, o), c)}, rd, wr)
+
+    def vcopy(out, a, rd, wr, c=SM):
+        op({"V": (lambda: g.vector.tensor_copy(out, a), c)}, rd, wr)
+
+    def copy(out, a, rd, wr, c):
+        op({"V": (lambda: g.vector.tensor_copy(out, a), c), "S": (f_act(out, a, F.Copy), c)}, rd, wr)
+
+    def shift(out, a, b, rd, wr, c):
+        op({"V": (f_ts(out, a, b, None, A.add, None), c), "S": (f_act(out, a, F.Identity, bias=b), c)}, rd, wr)
+
+    def fill(out, v, key, c=SM):
+        op({"V": (lambda: g.vector.memset(out, v), c)}, [], [key])
+
+    def act(out, a, fn, rd, wr, c=SM, **kw):
+        op({"S": (f_act(out, a, fn, **kw), c)}, rd, wr)
+
+    def mm(out, l, r, st, sp, rd, wr, c=PU):
+        op({"P": (lambda: g.tensor.matmul(out, l, r, st, sp), c)}, rd, wr)
+
+    def scan(out, data, add, init, rd, wr, c=SM):
+        op({"V": (lambda: g.vector.tensor_tensor_scan(out, data, add, init, A.add, A.add), c)}, rd, wr)
+
+    def total(out, a, rd, wr):
+        op({"V": (lambda: g.vector.tensor_reduce(out, a, AX.X, A.add), SM)}, rd, wr)
+
+    def iota(out, pat, base, cm, key, c, flag=True):
+        if flag:
+            op({"G": (lambda: g.iota(out, pat, base, cm, allow_small_or_imprecise_dtypes=True), c)}, [], [key])
+        else:
+            op({"G": (lambda: g.iota(out, pat, base, cm), c)}, [], [key])
+
+    acol, rcol, pcol, wcol, ecol, mcol = [T.col[:, j:j + 1] for j in range(6)]
+    mine = slice(16 * me, 16 * me + 16)
+
+    dmas("Y", "lsz", [(T.szi[:], T.sz[:])], [], ["szi"])
+    dmas("S", "lrf", [(T.rfi[:], T.rf[:])], [], ["rfi"])
+    dmas("Y", "sth", [(T.sh[:], T.rch[:])], [], ["sh"])
+    dmas("Y", "stc", [(T.sc[:], T.cd[:])], [], ["sc"])
+    dmas("Y", "stown", [(T.dc[me], T.cd[mine, :]), (T.dh[me], T.rch[mine, :])], [], ["down"])
+    iota(acol, [[1, 1]], -256, 1, "acol", 0.14)
+    iota(T.nn[:], [[1, 512]], -256, 0, "nn", 1.2)
+    iota(T.ai[:, 0:1], [[1, 1]], 0, 1, "ai0", 0.14, False)
+    iota(T.cb[:], [[1, 8], [0, 16]], 0, 0, "cb", 0.4)
+    iota(T.cp[:], [[0, 8], [1, 16]], 0, 0, "cp", 0.4)
+    fill(T.zero[:], 0.0, "zero", U)
+    fill(T.ll[:, 0:1], MID, "ll0")
+    fill(T.pre[:, 0:1], 0.0, "pre0")
+    fill(T.mid8[:], -MID, "mid8")
+    hot[0] = True
+    ts(T.ib[:], T.nn[:, 0:128], acol, None, A.is_equal, None, ["nn", "acol"], ["ib"])
+    ts(T.ih[:], T.nn[:, 0:128], acol, None, A.is_equal, None, ["nn", "acol"], ["ih"])
+    send("rc", lambda r: T.sh[r], T.dh[me], ["sh"], "dh", PLAN["msg"])
+    vcopy(T.szb[:], T.szi[:], ["szi"], ["szb"], U)
+    for j in range(4):
+        mm(T.pt0[:, j::4], T.szb[:, 128 * j:128 * j + 128], T.ib[:], True, True, ["szb", "ib"], ["pt0"], PU / 4)
+    act(T.ln[:], T.szb[:], F.Copy, ["szb"], ["ln", "tot0"], U, accum_out=T.tot0[:, 0:1])
+    ts(T.rfh[:], T.rfi[:], -2048.0, None, A.add, None, ["rfi"], ["rfh"], U)
+    for j in range(4):
+        mm(T.pt1[:, j::4], T.rfh[:, 128 * j:128 * j + 128], T.ih[:], True, True, ["rfh", "ih"], ["pt1"], PU / 4)
+    act(T.ms[:, 0::2, 4], T.zero[:, 0:64], F.Identity, ["zero", "tot0"], ["mshi"], bias=T.tot0[:, 0:1])
+    act(T.ms[:, :, 0:4], T.pt0[:], F.Copy, [], ["pt0", "ms"], U)
+    ts(T.ms[:, 1::2, 4], T.ms[:, 0::2, 4], -1.0, T.tot0[:, 0:1], A.mult, A.add, ["mshi", "tot0"], ["mslo"])
+    send("sz", lambda r: T.ms[:, 16 * r:16 * r + 16, :], T.ls[:, mine, :], ["ms", "mshi", "mslo"], "ls", PLAN["first"])
+    vcopy(T.mr[:], T.pt1[:], [], ["pt1", "mr"], U)
+    send("rf", lambda r: T.mr[:, 64 * r:64 * r + 64], T.lr[:, 64 * me:64 * me + 64], ["mr"], "lr", PLAN["first"] + 2.0)
+    act(T.ls[:, mine, :], T.ms[:, mine, :], F.Copy, ["ms", "mshi", "mslo"], ["lsown"])
+    vcopy(T.lr[:, 64 * me:64 * me + 64], T.mr[:, 64 * me:64 * me + 64], ["mr"], ["lrown"])
+    send("cd", lambda r: T.sc[r], T.dc[me], ["sc"], "dc", PLAN["first"] + 2.0)
+    dmas("Y", "lrc", [(T.rchi[:], T.dh[:])], ["dh", "down"], ["rchi"])
+    dmas("Y", "lcd", [(T.cdi[:], T.dc[:])], ["dc", "down"], ["cdi"])
+    hot[0] = False
+
+    ts(T.ai[:, 1:2], T.ai[:, 0:1], 4, None, A.arith_shift_right, None, ["ai0"], ["ai1"])
+    ts(T.ai[:, 2:3], T.ai[:, 0:1], 15, None, A.bitwise_and, None, ["ai0"], ["ai2"])
+    vcopy(T.col[:, 1:3], T.ai[:, 1:3], ["ai1", "ai2"], ["rp"])
+    ts(T.ee[:], T.cp[:], pcol, None, A.is_equal, None, ["cp", "rp"], ["ee"], 0.16)
+    ts(T.eq[:], T.nn[:, 0:8], 256.0, rcol, A.add, A.is_equal, ["nn", "rp"], ["eq"])
+    ts(T.lt[:], T.nn[:, 0:8], 256.0, rcol, A.add, A.is_gt, ["nn", "rp"], ["lt"])
+    ts(wcol, rcol, 16.0, 15.0, A.mult, A.add, ["rp"], ["wcol"])
+    ts(ecol, rcol, 128.0, pcol, A.mult, A.add, ["rp"], ["ecol"])
+    ts(mcol, pcol, 8.0, None, A.is_equal, None, ["rp"], ["mcol"])
+    ts(T.z8[:], T.nn[:, 0:8], 512.0, 256.0 * 512 + 256, A.mult, A.add, ["nn"], ["z8"])
+    for b in range(8):
+        act(T.sel[:, 128 * b:128 * b + 128], T.ee[:], F.Identity, ["ee", "eq"], ["sel%d" % b], 0.16, scale=T.eq[:, b:b + 1])
+    ts(T.uu[:], T.lt[:], 16777216.0, None, A.mult, None, ["lt"], ["uu"])
+    ts(T.mc[:], T.z8[:], mcol, None, A.mult, None, ["z8", "mcol"], ["mc"])
+    for c0, c1 in ((0, 512), (512, 1024), (1024, 1152)):
+        ts(T.we[:, c0:c1], T.nn[:, 0:c1 - c0], float(256 + c0 - 112), ecol, A.add, A.is_equal, ["nn", "ecol"], ["we%d" % c0], U / 2)
+    ts(T.wd[:], T.nn[:, 0:144], 256.0, wcol, A.add, A.is_equal, ["nn", "wcol"], ["wd"])
+    tt(T.uu[:], T.uu[:], T.eq[:], A.add, ["eq"], ["uu"])
+    ts(T.ni[:], T.nn[:, 0:128], acol, -1.0, A.is_equal, A.mult, ["nn", "acol"], ["ni"])
+    ts(T.ibig[:], T.nn[:, 0:128], acol, float(2 ** 41), A.is_equal, A.mult, ["nn", "acol"], ["ibig"])
+    ts(T.nib[:], T.nn[:, 0:128], acol, -float(2 ** 20), A.is_equal, A.mult, ["nn", "acol"], ["nib"])
+    ts(T.blk512[:], T.cb[:], rcol, 512.0, A.is_equal, A.mult, ["cb", "rp"], ["blk512"], 0.16)
+    ts(T.blk16[:], T.cb[:], rcol, 16.0, A.is_equal, A.mult, ["cb", "rp"], ["blk16"], 0.16)
+    ts(T.tmpc[:], T.cb[:], rcol, None, A.is_gt, None, ["cb", "rp"], ["tmpc"], 0.16)
+    tt(T.e2[:], T.tmpc[:], T.ee[:], A.mult, ["tmpc", "ee"], ["e2"], 0.3)
+    MW = ["mw%d" % b for b in range(8)]
+    for b in range(8):
+        o, col = T.mwin[:, 512 * b:512 * b + 512], T.mc[:, b:b + 1]
+        op({"V": (f_ts(o, T.nn[:], 0.0, col, A.mult, A.add), U / 2), "S": (f_act(o, T.zero[:], F.Identity, bias=col), U)}, ["nn", "zero", "mc"], [MW[b]])
+    vcopy(T.rchf[:], T.rchi[:], ["rchi"], ["rchf"])
+    ts(T.nrch[:], T.rchi[:], -1.0, None, A.mult, None, ["rchi"], ["nrch"])
+
+    TB = ["pt0", "pt1", "pt2", "pt3", "pf", "pm", "pt0", "pt1"]
+    BW = ["bw%d" % b for b in range(8)]
+
+    def table_mm(blocks, part):
+        for b in blocks:
+            mm(T[TB[b]][:], T.sel[:, 128 * b:128 * b + 128], T[part][:], part == "hi", part == "lo", ["sel%d" % b, part],
+               [TB[b]] + (["table"] if b == 7 else []))
+
+    def table_copy():
+        for b in range(8):
+            shift(T.bwin[:, 512 * b:512 * b + 512], T[TB[b]][:], T.bias[:, b:b + 1], ["bias"], [TB[b], BW[b]], U)
+            if b < 2:
+                table_mm([6 + b], "hi")
+                table_mm([6 + b], "lo")
+
+    hot[0] = True
+    for j in range(4):
+        mm(T.pr[:, 128 * j:128 * j + 128], T.ls[:, :, j], T.ib[:], True, True, ["ls", "lsown", "ib"], ["pr"], PU / 4)
+    scan(T.ll[:, 1:513], T.pr[:], T.zero[:], MID, ["zero"], ["pr", "ll"], U)
+    act(T.hi[:], T.ll[:, 0:512], F.Copy, ["ll", "ll0"], ["hi"], U)
+    tt(T.x8[:], T.ls[:, 0::16, 4], T.ls[:, 1::16, 4], A.add, ["ls", "lsown"], ["x8"])
+    scan(T.pre[:, 1:9], T.x8[:], T.zero[:, 0:8], 0.0, ["x8", "zero"], ["pre"])
+    ts(T.z8[:], T.x8[:], T.lt[:, me:me + 1], None, A.mult, None, ["x8", "lt"], ["z8"])
+    mm(T.pn[:, 0:8], T.ee[:], T.pre[:, 0:8], True, False, ["ee", "pre", "pre0"], ["pn"], PU / 2)
+    mm(T.pn[:, 0:8], T.ee[:], T.z8[:], False, True, ["ee", "z8"], ["pn"], PU / 2)
+    tt(T.lo[:], T.ll[:, 0:512], T.hi[:], A.subtract, ["ll", "ll0", "hi"], ["lo"], 2 * U)
+    table_mm(range(6), "hi")
+    table_mm(range(6), "lo")
+    tt(T.x8[:], T.pn[:, 0:8], T.eq[:], A.mult, ["eq"], ["pn", "x8"])
+    total(T.own[:, 0:1], T.x8[:], ["x8"], ["own"])
+    ts(T.bias[:], T.pn[:, 0:8], T.own[:, 0:1], None, A.subtract, None, ["own"], ["pn", "bias"])
+    table_copy()
+    for e in range(8):
+        for r in range(8):
+            c0 = 128 * e + 112 - 16 * r
+            mm(T.pn[:, e::8], T.we[:, c0:c0 + 128], T.lr[:, 64 * r:64 * r + 64], r == 0, r == 7, ["we0", "we512", "we1024", "lr", "lrown"], ["pn"], PU / 8)
+    ts(T.lst[:], T.pn[:], 2048.0, None, A.add, None, [], ["pn", "lst"], U)
+    hot[0] = False
+    copy(T.szr[:], T.pr[:], [], ["pr", "szr"], U)
+    for j in range(4):
+        mm(T.pr[:, 128 * j:128 * j + 128], T.lr[:, j::4], T.ih[:], True, True, ["lr", "lrown", "ih"], ["pr"], PU / 4)
+    vcopy(T.cdu[:], T.cdi[:], ["cdi"], ["cdu"])
+    act(T.cc[:], T.nn[:, 0:512].indirect(T.cdu[:, 0:32]), F.Copy, ["nn", "cdu"], ["cc"], GU)
+
+    def len_first(sz, dead, bank):
+        mm(T[bank][:], T.ib[:], T[sz][:], True, False, ["ib", sz], [bank])
+        mm(T[bank][:], T.ni[:], T[dead][:], False, False, ["ni", dead], [bank])
+
+    def len_last(far, out, bank, kw):
+        mm(T[bank][:], T.blk16[:], T[far][:], False, True, ["blk16", far], [bank])
+        act(T[out][:], T[bank][:], F.Relu, [], [bank, out] + (["totown"] if kw else []), U, **kw)
+
+    def deadw(j, out, bank):
+        mm(T[bank][:], T.ib[:], T[j][:], True, False, ["ib", j], [bank])
+        mm(T[bank][:], T.ni[:], T.nn[:], False, True, ["ni", "nn"], [bank])
+        act(T[out][:], T[bank][:], F.Relu, [], [bank, out], U, scale=-1024.0)
+
+    for t in range(1, RO + 1):
+        last = t == RO
+        src_m = "jj" if t == 1 else "mm"
+        if t > 1:
+            mm(T.pf[:], T.ibig[:], T.far[:], True, False, ["ibig", "far"], ["pf"])
+            mm(T.pf[:], T.nib[:], T.dead[:], False, False, ["nib", "dead"], ["pf"])
+
+        act(T.rr[:], T.pr[:], F.Identity, [], ["pr", "rr"], U, bias=2048.0 if t == 1 else 0.0)
+        if last:
+            dmas("Y", "str", [(T.sr[:], T.rr[:])], ["rr"], ["sr"])
+            dmas("Y", "rown", [(T.dr[me], T.rr[mine, :])], ["rr"], ["drown"])
+            send("ro", lambda r: T.sr[r], T.dr[me], ["sr"], "dr", PLAN["big"])
+        dmas("Y", "r%d" % t, [(T.r2[:], T.rr[:])], ["rr"], ["r2"])
+        tt(T.neq[:], T.rr[:, 0:512].indirect(T.cdu[:, 0:32]), T.r2[:], A.not_equal, ["rr", "r2", "cdu"], ["neq"], GU)
+        mm(T.pm[:], T.ib[:], T.cc[:], True, False, ["ib", "cc"], ["pm"])
+        mm(T.pm[:], T.blk512[:], T.neq[:], False, True, ["blk512", "neq"], ["pm"])
+        tt(T.jj[:], T.pm[:], T.nn[:], A.min, ["nn"], ["pm", "jj"], U)
+        if last:
+            dmas("Y", "stj", [(T.sj[:], T.jj[:])], ["jj"], ["sj"])
+            dmas("Y", "jown", [(T.dj[me], T.jj[mine, :])], ["jj"], ["djown"])
+            send("jo", lambda r: T.sj[r], T.dj[me], ["sj"], "dj", PLAN["big"])
+            dmas("Y", "yr", [(T.yr[:], T.dr[:])], ["dr", "drown"], [])
+            dmas("Y", "ljn", [(T.jn[:], T.dj[:])], ["dj", "djown"], ["jn"])
+            dmas("Y", "lj8", [(T.j8[0:8, :], T.dj[:, 0:8, :])], ["dj", "djown"], ["j8"])
+        else:
+            if t > 1:
+                act(T.mm[:], T.jj[:, 0:512].indirect(T.ml[:, 32 * (t - 2):32 * (t - 1)]), F.Copy, ["jj", "ml%d" % t], ["mm"], GU)
+            dmas("Y", "mw%d" % t, [(T.mwin[p::16, 512 * p:512 * p + 512], T[src_m][16 * p:16 * p + 8, :]) for p in range(8)], [src_m], MW)
+            for p in range(16):
+                mm(T.pn[:, 0:32], T.wd[:, 15 - p:143 - p], T[src_m][:, p::16], p == 0, p == 15, ["wd", src_m], ["pn"], PU / 8)
+            ts(T.ml[:, 32 * (t - 1):32 * t], T.pn[:, 0:32], 0.0625, 256.0, A.mult, A.add, [], ["pn", "ml%d" % (t + 1)])
+        deadw("jj", "dead", "pm")
+        len_first("szr", "dead", "pm")
+
+        dmas("Y", "l%d" % t, [(T.l2[:, 512 * j:512 * j + 512], T.ll[:, 0:512]) for j in range(2)], ["ll", "ll0"], ["l2"])
+
+        def gather(k, n):
+            tt(T.dd[:, 512 * k:512 * (k + n)], T.bwin[:, 0:4096].indirect(T.lst[:, 32 * k:32 * (k + n)]), T.l2[:, 0:512 * n], A.subtract,
+               BW + ["lst", "l2"], ["dd%d" % (k + j) for j in range(n)], n * GU - (n - 1) * 0.06)
+
+        def absol(k, n):
+            d = T.dd[:, 512 * k:512 * (k + n)]
+            act(d, d, F.Abs, [], ["dd%d" % (k + j) for j in range(n)], n * U)
+
+        def compare(k):
+            o, d = T.ind[:, 512 * k:512 * k + 512], T.dd[:, 512 * k:512 * k + 512]
+            op({"V": (f_ts(o, d, T.rchf[:, k:k + 1], None, A.is_gt, None), U), "S": (f_act(o, d, F.Relu, bias=T.nrch[:, k:k + 1]), U)},
+               ["dd%d" % k, "rchf", "nrch"], ["ind%d" % k])
+            mm(T.pf[:], T.wd[:, 15 - k:143 - k], o, t == 1 and k == 0, k == 15, ["wd", "ind%d" % k], ["pf"])
+
+        for q in range(8 + PLAN["lag"]):
+            hot[0] = q >= 7
+            if q in (0, 7):
+                for k in (2 * q, 2 * q + 1):
+                    gather(k, 1)
+                    absol(k, 1)
+            elif q < 7:
+                gather(2 * q, 2)
+                absol(2 * q, 2)
+            if q >= PLAN["lag"]:
+                compare(2 * (q - PLAN["lag"]))
+                compare(2 * (q - PLAN["lag"]) + 1)
+
+        hot[0] = True
+        ts(T.far[:], T.pf[:], 0.0, None, A.is_gt, None, [], ["pf", "far"], U)
+        if not last:
+            slot = (8 * (t - 1) + me) * 4
+            tcol = T.tot[:, slot:slot + 1]
+            lists_t = T.ml[:, 32 * (t - 1):32 * t]
+            len_last("far", "ln", "pm", {"accum_out": tcol})
+            send("t%d" % t, lambda r: tcol, tcol, ["totown"], "tot%d" % t, PLAN["msg"])
+            scan(T.ll[:, 1:513], T.ln[:], T.zero[:], MID, ["ln", "zero"], ["ll"], U)
+            act(T.hi[:], T.ll[:, 0:512].indirect(lists_t), F.Copy, ["ll", "ll0", "ml%d" % (t + 1)], ["hi"], GU)
+            tt(T.lo[:], T.ll[:, 0:512].indirect(lists_t), T.hi[:], A.subtract, ["ll", "ll0", "hi", "ml%d" % (t + 1)], ["lo"], GU)
+            scan(T.pre[:, 1:9], T.tot[:, 32 * (t - 1):32 * t:4], T.zero[:, 0:8], 0.0, ["tot%d" % t, "totown", "zero"], ["pre"])
+            mm(T.pn[:, 8:9], T.e2[:], T.pre[:, 8:9], True, True, ["e2", "pre"], ["pn"], PU / 2)
+            if me == 0:
+                ts(T.z8[:], T.lt[:], T.pre[:, 8:9], None, A.mult, None, ["lt", "pre"], ["z8"])
+            else:
+                ts(T.z8[:], T.uu[:], T.pre[:, me:me + 1], T.pre[:, 8:9], A.mult, A.min, ["uu", "pre"], ["z8"])
+            mm(T.pn[:, 0:8], T.ee[:], T.z8[:], True, True, ["ee", "z8"], ["pn"], PU / 2)
+            ts(T.bias[:], T.pn[:, 0:8], T.pn[:, 8:9], T.pre[:, me:me + 1], A.subtract, A.subtract, ["pre", "pre0"], ["pn", "bias"])
+            table_mm(range(6), "hi")
+            table_mm(range(6), "lo")
+            table_copy()
+            hot[0] = False
+            for k in range(16):
+                o = T.gr[:, 512 * k:512 * k + 512]
+                src = T.mwin[:, 0:4096].indirect(T.lst[:, 32 * k:32 * k + 32])
+                if k < PLAN["both"]:
+                    copy(o, src, MW + ["lst"], ["gr%d" % k], GU)
+                else:
+                    act(o, src, F.Copy, MW + ["lst"], ["gr%d" % k], GU)
+                mm(T.pr[:], T.wd[:, 15 - k:143 - k], o, k == 0, k == 15, ["wd", "gr%d" % k] + (["table"] if k >= PLAN["early"] else []), ["pr"])
+        else:
+            tcol = T.tot0[:, 4:5]
+            len_last("far", "ln", "pm", {"accum_out": tcol})
+            for j in range(4):
+                mm(T.pt0[:, j::4], T.far[:, 128 * j:128 * j + 128], T.ib[:], True, True, ["far", "ib"], ["pt0"], PU / 4)
+            vcopy(T.ft[:, :, 0:4], T.pt0[:], [], ["pt0", "ft"], U)
+            ts(T.ft[:, 0::2, 4], T.zero[:, 0:64], tcol, MID, A.add, A.add, ["zero", "totown"], ["fthi"])
+            ts(T.own[:, 2:3], tcol, MID, None, A.add, None, ["totown"], ["own2"])
+            ts(T.ft[:, 1::2, 4], T.ft[:, 0::2, 4], -1.0, T.own[:, 2:3], A.mult, A.add, ["fthi", "own2"], ["ftlo"])
+            send("fo", lambda r: T.ft[:, 16 * r:16 * r + 16, :], T.lf[:, mine, :], ["ft", "fthi", "ftlo"], "lf", PLAN["msg"] + 1.0)
+            vcopy(T.lf[:, mine, :], T.ft[:, mine, :], ["ft", "fthi", "ftlo"], ["lfown"])
+            mm(T.pn[:], T.ib[:], T.jn[:], True, False, ["ib", "jn", "ft"], ["pn"])
+            mm(T.pn[:], T.ni[:], T.nn[:], False, True, ["ni", "nn"], ["pn"])
+            act(T.deadn[:], T.pn[:], F.Relu, [], ["pn", "deadn"], U, scale=-1024.0)
+            act(T.j8f[0:8, :], T.j8[0:8, :], F.Identity, ["j8", "deadn"], ["j8f"], U, bias=float(256 + S * me))
+            dmas("Y", "yj", [(T.yj[:], T.j8f[0:8, :])], ["j8f"], [])
+            len_first("szb", "deadn", "pt3")
+            for p in ("pt1", "pt2"):
+                for j in range(4):
+                    mm(T[p][:, 128 * j:128 * j + 128], T.lf[:, :, j], T.ib[:], True, True, ["lf", "lfown", "ib"], [p], PU / 4)
+            act(T.farn[:], T.pt1[:], F.Copy, [], ["pt1", "farn"], U)
+            tt(T.x8[:], T.lf[:, 0::16, 4], T.lf[:, 1::16, 4], A.add, ["lf", "lfown"], ["x8"])
+            scan(T.pre[:, 1:9], T.x8[:], T.mid8[:], 0.0, ["x8", "mid8"], ["pre"])
+            ts(T.own[:, 1:2], T.pre[:, 8:9], T.lt[:, me:me + 1], None, A.mult, None, ["pre", "lt"], ["own1"])
+            ts(T.z8[:], T.pre[:, 0:8], T.eq[:, me:me + 1], T.own[:, 1:2], A.mult, A.add, ["pre", "pre0", "eq", "own1"], ["z8"])
+            mm(T.pn[:, 0:8], T.ee[:], T.z8[:], True, True, ["ee", "z8"], ["pn"], PU / 2)
+            len_last("farn", "lnn", "pt3", {})
+            tt(T.x8[:], T.pn[:, 0:8], T.eq[:], A.mult, ["eq"], ["pn", "x8"])
+            total(T.la[:, 0:1], T.x8[:], ["x8"], ["la0"])
+            scan(T.la[:, 1:512], T.lnn[:, 0:511], T.zero[:, 0:511], T.la[:, 0:1], ["lnn", "la0", "zero"], ["la"], U)
+            dmas("Y", "ya", [(T.ya[:], T.la[:, 0:512])], ["la", "la0"], [])
+            vcopy(T.yfb[:], T.pt2[:], [], ["pt2", "yfb"], U)
+            dmas("S", "yf", [(T.yf[:], T.yfb[:])], ["yfb"], [])
+
+    count = {"V": 0, "S": 0, "P": 0, "G": 0}
+    seen = {q: {} for q in Q}
+    token, most = {}, {}
+    for i, q in place(calls):
+        c = calls[i]
+        if q != "-":
+            want = {}
+            for d in c["deps"]:
+                s, v = token[d]
+                if (s == "P" and q == "P") or (q == "G" and s.startswith("o_")):
+                    continue
+                want[s] = max(want.get(s, 0), v)
+            for s, v in want.items():
+                if seen[q].get(s, 0) < v:
+                    Q[q].wait_ge(T.sem[s], v)
+                    seen[q][s] = v
+            made = c["alts"][q][0]()
+            if c["tok"] is None:
+                count[q] += 1
+                made.then_inc(T.sem[q], 1)
+        token[i] = c["tok"] or (q, count[q])
+        most[token[i][0]] = max(most.get(token[i][0], 0), token[i][1])
+    for s, v in most.items():
+        if max(seen[q].get(s, 0) for q in seen) < v:
+            g.wait_ge(T.sem[s], v)

@@ -3,8 +3,16 @@ from concourse.mybir import AluOpType as A, ActivationFunctionType as F, AxisLis
 
 N, S, RO = 8, 512, 4
 MID = -131072.0
+LIFT = 98304.0
+EDGE = 2.0 - 2.0 ** -6
+TURN = 2.0 - 3 * 2.0 ** -8
 
-PLAN = {"U": 0.56, "G": 0.89, "P": 0.27, "s": 0.1, "dma": 2.6, "msg": 5.0, "first": 8.0, "big": 9.0, "lag": 2, "hold": 0.7, "both": 13, "early": 3}
+PLAN = {"U": 0.52, "G": 0.8, "P": 0.35, "s": 0.12, "dma": 2.6, "msg": 3.6, "first": 6.0, "big": 7.0,
+        "lag": 3, "neq": "S", "passes": 150, "moves": 4000, "spare": (0.0, 0.2, 0.5, 1.0, 2.0), "shake": 0.5}
+CASES = ((1.0, 1.0, 1.0), (0.7, 1.28, 1.0), (1.2, 0.75, 1.0), (0.8, 1.1, 1.4))
+GATHERS = (1, 1, 2, 2, 2, 2, 2, 1, 1, 1, 1)
+RENAMES = (3, 3, 2, 2, 2, 2, 1, 1)
+OVER = ["S" * n + "V" * (16 - n) for n in (7, 5, 5, 7)]
 
 f32, bf, h16, i32, u16 = "float32", "bfloat16", "float16", "int32", "uint16"
 
@@ -14,33 +22,40 @@ def _sb(n, d):
 
 
 SCRATCH = {
-    "szi": _sb(512, i32), "rfi": _sb(512, i32), "szb": _sb(512, bf), "rfh": _sb(512, h16),
-    "ms": ("sbuf", [128, 128, 5], bf), "ls": ("sbuf", [128, 128, 5], bf), "mr": _sb(512, h16), "lr": _sb(512, h16),
-    "sc": ("dram", [8, 128, 4], i32), "dc": ("dram", [8, 128, 4], i32), "sh": ("dram", [8, 128, 2], i32), "dh": ("dram", [8, 128, 2], i32),
-    "cdi": _sb(32, i32), "rchi": _sb(16, i32), "cdu": _sb(32, u16), "rchf": _sb(16, f32), "nrch": _sb(16, f32),
-    "nn": _sb(512, bf), "zero": _sb(512, f32), "ai": _sb(4, i32), "col": _sb(16, f32),
+    "szi": _sb(512, i32), "rfi": _sb(512, i32), "rfj": _sb(512, i32), "cdo": _sb(32, i32), "cdv": _sb(32, u16),
+    "szb": _sb(512, bf), "rfh": _sb(512, h16), "rko": _sb(512, bf), "rkp": _sb(512, bf), "jc": _sb(1024, bf),
+    "ms": ("sbuf", [128, 128, 5], bf), "ls": ("sbuf", [128, 128, 5], bf), "mr": ("sbuf", [128, 8, 64], h16), "lso": _sb(512, u16),
+    "sh": ("dram", [8, 128, 8], i32), "dh": ("dram", [8, 128, 8], i32), "sc": ("dram", [8, 128, 8], bf), "dc": ("dram", [8, 128, 8], bf),
+    "dl": ("dram", [8, 128, 64], u16),
+    "cdi": _sb(32, i32), "rchi": _sb(16, i32), "cdu": _sb(32, u16),
+    "rl": _sb(512, bf), "rl2": _sb(512, bf), "hc": _sb(512, bf), "lc": _sb(512, bf),
+    "nn": _sb(512, bf), "zero": _sb(512, f32), "ai": _sb(4, i32), "col": _sb(16, f32), "one": _sb(8, bf),
     "cb": _sb(128, f32), "cp": _sb(128, f32), "tmpc": _sb(128, f32),
-    "ib": _sb(128, bf), "ih": _sb(128, h16), "ni": _sb(128, bf), "ibig": _sb(128, bf), "nib": _sb(128, bf),
+    "ib": _sb(128, bf), "ih": _sb(128, h16), "ni": _sb(128, bf), "nk": _sb(128, bf), "ng": _sb(128, bf), "old": _sb(128, bf),
+    "pb0": _sb(128, bf), "pk": _sb(128, bf), "pg": _sb(128, bf), "dgo": _sb(128, bf), "wb": _sb(256, bf),
+    "rchf": _sb(16, f32), "rec": _sb(16, f32), "scl": _sb(16, f32), "steps": _sb(16, f32),
+    "cand": ("sbuf", [128, 16, 16], f32), "fits": ("sbuf", [128, 16, 16], f32),
     "blk512": _sb(128, bf), "blk16": _sb(128, bf), "ee": _sb(128, f32), "e2": _sb(128, f32),
     "wd": _sb(144, bf), "we": _sb(1152, h16), "sel": _sb(1024, bf),
-    "eq": _sb(8, f32), "lt": _sb(8, f32), "uu": _sb(8, f32), "mc": _sb(8, f32), "mid8": _sb(8, f32),
+    "eq": _sb(8, f32), "lt": _sb(8, f32), "uu": _sb(8, f32),
     "tot0": _sb(8, f32), "x8": _sb(8, f32), "z8": _sb(8, f32), "pre": _sb(16, f32), "bias": _sb(8, f32), "own": _sb(8, f32),
     "tot": _sb(96, f32),
-    "szr": _sb(512, bf), "ll": _sb(520, f32), "l2": _sb(1024, f32), "ln": _sb(512, f32), "hi": _sb(512, bf), "lo": _sb(512, bf),
+    "szr": _sb(512, bf), "ll": _sb(1024, f32), "ln": _sb(512, f32),
     "lst": _sb(512, u16), "ml": _sb(96, u16), "bwin": _sb(4096, f32), "mwin": _sb(4096, bf),
     "dd": _sb(8192, f32), "ind": _sb(8192, bf), "gr": _sb(8192, bf),
-    "rr": _sb(512, f32), "r2": _sb(512, f32), "neq": _sb(512, bf), "cc": _sb(512, bf), "jj": _sb(512, bf), "mm": _sb(512, bf),
-    "dead": _sb(512, bf), "far": _sb(512, bf),
-    "sr": ("dram", [8, 128, 64], f32), "dr": ("dram", [8, 128, 64], f32),
-    "sj": ("dram", [8, 128, 64], bf), "dj": ("dram", [8, 128, 64], bf),
-    "jn": _sb(512, bf), "j8": _sb(512, bf), "j8f": _sb(512, f32), "deadn": _sb(512, bf),
-    "ft": ("sbuf", [128, 128, 5], bf), "lf": ("sbuf", [128, 128, 5], bf),
-    "farn": _sb(512, bf), "yfb": _sb(512, f32), "lnn": _sb(512, f32), "la": _sb(520, f32),
+    "neq": _sb(512, bf), "cc": _sb(512, bf), "j1": _sb(512, bf), "jj": _sb(512, bf), "mm": _sb(512, bf), "far": _sb(512, bf),
+    "sr": ("dram", [8, 128, 64], bf), "dr": ("dram", [8, 128, 64], bf),
+    "sj": ("dram", [8, 128, 4], bf), "dj": ("dram", [8, 128, 4], bf),
+    "rn": _sb(512, bf), "rr": _sb(512, f32), "jn": _sb(512, bf), "j8": _sb(512, bf), "j8f": _sb(512, f32),
+    "alv": _sb(512, bf), "sza": _sb(512, bf), "ft": ("sbuf", [128, 128, 5], bf), "lf": ("sbuf", [128, 128, 5], bf),
+    "farn": _sb(512, bf), "yfb": _sb(512, f32), "la": _sb(520, f32),
     "pf": ("psum", [128, 512], f32), "pr": ("psum", [128, 512], f32), "pm": ("psum", [128, 512], f32), "pn": ("psum", [128, 512], f32),
     "pt0": ("psum", [128, 512], f32), "pt1": ("psum", [128, 512], f32), "pt2": ("psum", [128, 512], f32), "pt3": ("psum", [128, 512], f32),
 }
-_MSG = ["rc", "cd", "sz", "rf", "t1", "t2", "t3", "ro", "jo", "fo"]
-_DMA = ["lsz", "lrf", "sth", "stc", "stown", "lrc", "lcd", "mw1", "mw2", "mw3", "r1", "r2", "r3", "r4", "l1", "l2", "l3", "l4", "str", "rown", "stj", "jown", "yr", "ljn", "lj8", "yj", "yf", "ya"]
+_MSG = ["rc", "sz", "rf", "jc", "t1", "t2", "t3", "ro", "jo", "fo"]
+_DMA = (["lsz", "lrf", "lrg", "lco", "sth", "stown", "lrc", "lcd", "stc", "cown", "lj1", "lcc", "lown", "lst",
+         "str", "rown", "stj", "jown", "lrn", "yr", "ljn", "lj8", "yj", "yf", "ya"]
+        + [a + str(t) for a in ("mw", "r", "q", "l") for t in range(1, RO + 1)])
 SEMAPHORES = ["V", "S", "P", "G"] + ["a_" + m for m in _MSG] + ["o_" + m for m in _MSG] + ["d_" + d for d in _DMA]
 
 
@@ -73,59 +88,116 @@ def engine_split(src, cores, topo):
 
 def place(calls):
     n = len(calls)
-    end, queue, order = [None] * n, [None] * n, []
-    free = {q: 0.0 for q in "VSPGY-"}
+    deps = [c["deps"] for c in calls]
     users = [[] for _ in range(n)]
-    left = [len(c["deps"]) for c in calls]
-    for i, c in enumerate(calls):
-        for d in c["deps"]:
+    for i in range(n):
+        for d in deps[i]:
             users[d].append(i)
-    cand = set(i for i in range(n) if left[i] == 0)
 
-    def ready(i, q):
-        return max([end[d] + (0.0 if q == "P" and queue[d] == "P" or q == "-" else PLAN["s"]) for d in calls[i]["deps"]] + [0.0])
-
-    def soon(i, depth):
-        t = 0.0
-        for d in calls[i]["deps"]:
-            if end[d] is not None:
-                t = max(t, end[d] + PLAN["s"])
-            elif depth == 0:
-                return 1e9
-            else:
-                q, (_, c) = min(calls[d]["alts"].items())
-                t = max(t, max(soon(d, depth - 1), free[q] if q == "P" else 0.0) + c + calls[d]["lat"] + PLAN["s"])
-        return t
-
-    while cand:
-        best = None
-        for i in cand:
-            for q in calls[i]["alts"]:
-                key = (max(free[q], ready(i, q)) if q != "-" else ready(i, q), i, q)
-                if best is None or key < best:
-                    best = key
-        t, i, q = best
-        if q in "VS" and calls[i]["alts"][q][1] > 0.3:
-            wait = None
-            for j in range(max(0, i - 120), i):
-                if end[j] is None and calls[j]["hot"] and q in calls[j]["alts"]:
-                    tj = soon(j, 3)
-                    if t < tj <= t + PLAN["hold"]:
-                        wait = tj if wait is None else min(wait, tj)
-            if wait is not None:
-                free[q] = wait + 1e-6
-                continue
-        cand.remove(i)
+    def time(i, q, case):
         c = calls[i]["alts"][q][1]
-        if q != "-":
-            free[q] = t + c
-        end[i], queue[i] = t + c + calls[i]["lat"], q
-        order.append((i, q))
-        for u in users[i]:
-            left[u] -= 1
-            if left[u] == 0:
-                cand.add(u)
+        return c * (case[0] if q == "P" else case[1] if q in "VS" and c >= PLAN["G"] else 1.0)
+
+    def sweep(before, after, urgency, back, case, spare):
+        start, end, queue = [0.0] * n, [0.0] * n, [None] * n
+        busy = {q: [] for q in "VSPGY"}
+        left = [len(b) for b in before]
+        cand = [i for i in range(n) if left[i] == 0]
+        while cand:
+            i = min(cand, key=lambda j: urgency[j])
+            cand.remove(i)
+            best = None
+            for q in calls[i].get("first", calls[i]["alts"]):
+                t, c = 0.0, time(i, q, case)
+                for d in before[i]:
+                    later = queue[d] if back else q
+                    gap = 0.0 if later == "-" or (q == "P" and queue[d] == "P") else PLAN["s"]
+                    t = max(t, end[d] + gap + calls[i if back else d]["lat"] * case[2])
+                at = 0
+                if q != "-":
+                    row = busy[q]
+                    at = len(row)
+                    while at > 0 and row[at - 1][1] > t:
+                        at -= 1
+                    while at < len(row) and row[at][0] < t + c - 1e-9:
+                        t = max(t, row[at][1])
+                        at += 1
+                key = t + c + (spare if q == "V" else 0.0)
+                if best is None or key < best[0] - 1e-9:
+                    best = (key, t + c, t, q, at)
+            _, end[i], start[i], queue[i], at = best
+            if queue[i] != "-":
+                busy[queue[i]].insert(at, (start[i], end[i]))
+            for u in after[i]:
+                left[u] -= 1
+                if left[u] == 0:
+                    cand.append(u)
+        return start, end, queue
+
+    cost = [{q: [(time(i, q, case), calls[i]["lat"] * case[2]) for case in CASES] for q in calls[i]["alts"]} for i in range(n)]
+
+    def run(order, k):
+        end, free, onp, s = [0.0] * n, dict.fromkeys("VSPGY-", 0.0), [False] * n, PLAN["s"]
+        last, why = dict.fromkeys("VSPGY-", -1), [None] * n
+        for i, q in order:
+            t, by, own = (free[q], last[q], True) if q != "-" else (0.0, -1, False)
+            onp[i] = q == "P"
+            for d in deps[i]:
+                e = end[d] if q == "-" or (onp[i] and onp[d]) else end[d] + s
+                if e >= t:
+                    t, by, own = e, d, False
+            c, lat = cost[i][q][k]
+            free[q], last[q] = t + c, i
+            end[i], why[i] = t + c + lat, (by, own)
+        return end, why
+
+    def score(order):
+        return sum(max(run(order, k)[0]) for k in range(len(CASES)))
+
+    seed = [1]
+
+    def pick(m):
+        seed[0] = (seed[0] * 1103515245 + 12345) % 2 ** 31
+        return (seed[0] >> 8) % m
+
+    urgency, best = [c["rank"] for c in calls], None
+    for p in range(PLAN["passes"]):
+        case, spare = CASES[p // 3 % len(CASES)], PLAN["spare"][p // 3 % len(PLAN["spare"])]
+        start, end, queue = sweep(deps, users, urgency, False, case, spare)
+        done = [end[i] + calls[i]["lat"] for i in range(n)]
+        order = [(i, queue[i]) for i in sorted(range(n), key=lambda j: (start[j], j))]
+        if best is None or score(order) < best[0]:
+            best = (score(order), order, done)
+        if p % 3 == 2:
+            done = [e + PLAN["shake"] * pick(1000) / 1000 for e in best[2]]
+        urgency = [-e for e in sweep(users, deps, [-e for e in done], True, case, spare)[1]]
+
+    now, order = best[0], best[1]
+    for step in range(PLAN["moves"]):
+        end, why = run(order, step % len(CASES))
+        i, pairs = max(range(n), key=lambda j: end[j]), []
+        while i >= 0:
+            if why[i][1] and why[i][0] >= 0:
+                pairs.append((why[i][0], i))
+            i = why[i][0]
+        at = {j: p for p, (j, _) in enumerate(order)}
+        for _ in range(8):
+            (u, v), how = pairs[pick(len(pairs))], pick(4)
+            i = v if how % 2 == 0 else u
+            q, to = order[at[i]][1], (at[u] - 4 * pick(3), at[v] + 6 * pick(4), at[i] + pick(31) - 15, at[i] + pick(31) - 15)[how]
+            if how >= 2:
+                q = [o for o in calls[i]["alts"] if o != q or len(calls[i]["alts"]) == 1][0]
+            to = min([at[w] - 1 for w in users[i]] + [max([at[d] + 1 for d in deps[i]] + [to, 0])])
+            new = order[:at[i]] + order[at[i] + 1:]
+            new.insert(to, (i, q))
+            tried = score(new)
+            if tried <= now:
+                now, order = tried, new
+                break
     return order
+
+
+ORDER = []
 
 
 def rank_program(g, core, T, topo):
@@ -134,12 +206,12 @@ def rank_program(g, core, T, topo):
         return
     cores = list(T.cores)
     Q = {"V": g.vector, "S": g.scalar, "P": g.tensor, "G": g, "Y": g.sync}
-    U, GU, PU, SM = PLAN["U"], PLAN["G"], PLAN["P"], PLAN["s"]
+    U, GU, PU, SM = PLAN["U"], PLAN["G"], PLAN["P"], 0.07
     split = engine_split(core, cores, topo)
     arrive = sum(len(engine_split(c, cores, topo)[core]) for c in cores if c != core)
     nsent = sum(len(v) for v in split.values())
 
-    calls, writer, readers, hot = [], {}, {}, [False]
+    calls, writer, readers, later = [], {}, {}, [0]
 
     def op(alts, rd, wr, lat=0.0, tok=None, more=()):
         deps = set(more)
@@ -151,7 +223,7 @@ def rank_program(g, core, T, topo):
                 deps.add(writer[k])
             deps.update(readers.get(k, []))
         i = len(calls)
-        calls.append({"alts": alts, "deps": sorted(deps), "lat": lat, "tok": tok, "hot": hot[0]})
+        calls.append({"alts": alts, "deps": sorted(deps), "lat": lat, "tok": tok, "wr": wr, "rank": i + later[0]})
         for k in rd:
             readers.setdefault(k, []).append(i)
         for k in wr:
@@ -210,6 +282,10 @@ def rank_program(g, core, T, topo):
     def mm(out, l, r, st, sp, rd, wr, c=PU):
         op({"P": (lambda: g.tensor.matmul(out, l, r, st, sp), c)}, rd, wr)
 
+    def sums(bank, terms, st=True, sp=True):
+        for j, (w, v) in enumerate(terms):
+            mm(T[bank][:], T[w][:], T[v][:], st and j == 0, sp and j == len(terms) - 1, [w, v], [bank])
+
     def scan(out, data, add, init, rd, wr, c=SM):
         op({"V": (lambda: g.vector.tensor_tensor_scan(out, data, add, init, A.add, A.add), c)}, rd, wr)
 
@@ -222,24 +298,26 @@ def rank_program(g, core, T, topo):
         else:
             op({"G": (lambda: g.iota(out, pat, base, cm), c)}, [], [key])
 
-    acol, rcol, pcol, wcol, ecol, mcol = [T.col[:, j:j + 1] for j in range(6)]
+    def many(n):
+        return n * GU - (n - 1) * 0.06
+
+    acol, rcol, pcol, wcol, ecol, mcol, ocol, lecol = [T.col[:, j:j + 1] for j in range(8)]
     mine = slice(16 * me, 16 * me + 16)
 
     dmas("Y", "lsz", [(T.szi[:], T.sz[:])], [], ["szi"])
     dmas("S", "lrf", [(T.rfi[:], T.rf[:])], [], ["rfi"])
-    dmas("Y", "sth", [(T.sh[:], T.rch[:])], [], ["sh"])
-    dmas("Y", "stc", [(T.sc[:], T.cd[:])], [], ["sc"])
-    dmas("Y", "stown", [(T.dc[me], T.cd[mine, :]), (T.dh[me], T.rch[mine, :])], [], ["down"])
+    dmas("Y", "sth", [(T.sh[:, 0:32, :], T.rch[:]), (T.sh[:, 32:96, :], T.cd[:]), (T.sh[:, 96:128, :], T.rch[:])], [], ["sh"])
+    dmas("S", "lco", [(T.cdo[:], T.cd[:])], [], ["cdo"])
+    dmas("S", "lrg", [(T.rfj[:], T.rf[:])], [], ["rfj"])
+    dmas("Y", "stown", [(T.dh[me, 32:96, :], T.cd[mine, :]), (T.dh[me, 0:32, :], T.rch[mine, :])], [], ["down"])
     iota(acol, [[1, 1]], -256, 1, "acol", 0.14)
     iota(T.nn[:], [[1, 512]], -256, 0, "nn", 1.2)
     iota(T.ai[:, 0:1], [[1, 1]], 0, 1, "ai0", 0.14, False)
     iota(T.cb[:], [[1, 8], [0, 16]], 0, 0, "cb", 0.4)
     iota(T.cp[:], [[0, 8], [1, 16]], 0, 0, "cp", 0.4)
     fill(T.zero[:], 0.0, "zero", U)
-    fill(T.ll[:, 0:1], MID, "ll0")
     fill(T.pre[:, 0:1], 0.0, "pre0")
-    fill(T.mid8[:], -MID, "mid8")
-    hot[0] = True
+    fill(T.one[:], 1.0, "one")
     ts(T.ib[:], T.nn[:, 0:128], acol, None, A.is_equal, None, ["nn", "acol"], ["ib"])
     ts(T.ih[:], T.nn[:, 0:128], acol, None, A.is_equal, None, ["nn", "acol"], ["ih"])
     send("rc", lambda r: T.sh[r], T.dh[me], ["sh"], "dh", PLAN["msg"])
@@ -255,235 +333,256 @@ def rank_program(g, core, T, topo):
     ts(T.ms[:, 1::2, 4], T.ms[:, 0::2, 4], -1.0, T.tot0[:, 0:1], A.mult, A.add, ["mshi", "tot0"], ["mslo"])
     send("sz", lambda r: T.ms[:, 16 * r:16 * r + 16, :], T.ls[:, mine, :], ["ms", "mshi", "mslo"], "ls", PLAN["first"])
     vcopy(T.mr[:], T.pt1[:], [], ["pt1", "mr"], U)
-    send("rf", lambda r: T.mr[:, 64 * r:64 * r + 64], T.lr[:, 64 * me:64 * me + 64], ["mr"], "lr", PLAN["first"] + 2.0)
-    act(T.ls[:, mine, :], T.ms[:, mine, :], F.Copy, ["ms", "mshi", "mslo"], ["lsown"])
-    vcopy(T.lr[:, 64 * me:64 * me + 64], T.mr[:, 64 * me:64 * me + 64], ["mr"], ["lrown"])
-    send("cd", lambda r: T.sc[r], T.dc[me], ["sc"], "dc", PLAN["first"] + 2.0)
-    dmas("Y", "lrc", [(T.rchi[:], T.dh[:])], ["dh", "down"], ["rchi"])
-    dmas("Y", "lcd", [(T.cdi[:], T.dc[:])], ["dc", "down"], ["cdi"])
-    hot[0] = False
-
     ts(T.ai[:, 1:2], T.ai[:, 0:1], 4, None, A.arith_shift_right, None, ["ai0"], ["ai1"])
     ts(T.ai[:, 2:3], T.ai[:, 0:1], 15, None, A.bitwise_and, None, ["ai0"], ["ai2"])
     vcopy(T.col[:, 1:3], T.ai[:, 1:3], ["ai1", "ai2"], ["rp"])
+    ts(ecol, rcol, 17.0, pcol, A.mult, A.add, ["rp"], ["ecol"])
+    ts(ecol, ecol, 8.0, 7.0 - 256.0, A.mult, A.add, [], ["ecol"])
+    for c0, c1 in ((0, 512), (512, 1024), (1024, 1088)):
+        ts(T.we[:, c0:c1], T.nn[:, 0:c1 - c0], float(c0), ecol, A.add, A.is_equal, ["nn", "ecol"], ["we%d" % c0], U / 2)
+    for e in range(8):
+        for u in range(8):
+            c0 = 136 * e + 7 - u
+            mm(T.pr[:, e::8], T.we[:, c0:c0 + 128], T.mr[:, :, 8 * u:8 * u + 8], u == 0, u == 7, ["we0", "we512", "we1024", "mr"], ["pr"], PU / 8)
+    ts(T.lso[:], T.pr[:], 2048.0, None, A.add, None, [], ["pr", "lso"], U)
+    send("rf", lambda r: T.lso[:, 64 * r:64 * r + 64], T.dl[me], ["lso"], "dl", PLAN["first"])
+    dmas("Y", "lown", [(T.dl[me], T.lso[:, 64 * me:64 * me + 64])], ["lso"], ["dlown"])
+    dmas("Y", "lst", [(T.lst[:], T.dl[:])], ["dl", "dlown"], ["lst"])
+    act(T.ls[:, mine, :], T.ms[:, mine, :], F.Copy, ["ms", "mshi", "mslo"], ["lsown"])
+    dmas("Y", "lrc", [(T.rchi[:], T.dh[:, 0:32, :])], ["dh", "down"], ["rchi"])
+    dmas("Y", "lcd", [(T.cdi[:], T.dh[:, 32:96, :])], ["dh", "down"], ["cdi"])
+
+    ts(T.blk512[:], T.cb[:], rcol, 512.0, A.is_equal, A.mult, ["cb", "rp"], ["blk512"], 0.16)
+    vcopy(T.cdv[:], T.cdo[:], ["cdo"], ["cdv"])
+    act(T.mm[:], T.nn[:, 0:512].indirect(T.cdv[:, 0:32]), F.Copy, ["nn", "cdv"], ["mm"], GU)
+    tt(T.neq[:], T.rfi[:, 0:512].indirect(T.cdv[:, 0:32]), T.rfj[:], A.not_equal, ["rfi", "rfj", "cdv"], ["neq"], GU)
+    sums("pt2", [("ib", "mm"), ("blk512", "neq")])
+    tt(T.jc[:, 0:512], T.pt2[:], T.nn[:], A.min, ["nn"], ["pt2", "jc0"], U)
+    shift(T.rko[:], T.rfh[:], 2048.0 - 255.5 + LIFT, ["rfh"], ["rko"], U)
+    copy(T.rkp[:], T.rko[:], ["rko"], ["rkp"], U)
+    tt(T.rl[:], T.rko[:, 0:512].indirect(T.cdv[:, 0:32]), T.rkp[:], A.not_equal, ["rko", "rkp", "cdv"], ["rl"], GU)
+    sums("pt3", [("ib", "mm"), ("blk512", "rl")])
+    ts(T.jc[:, 512:1024], T.pt3[:], 512.0, None, A.min, None, [], ["pt3", "jc1"], U)
+    dmas("Y", "stc", [(T.sc[:], T.jc[0::16, :])], ["jc0", "jc1"], ["sc"])
+    dmas("Y", "cown", [(T.dc[me], T.jc[16 * me:16 * me + 1, :])], ["jc0", "jc1"], ["dcown"])
+    send("jc", lambda r: T.sc[r], T.dc[me], ["sc"], "dc", PLAN["msg"])
+
+    fill(T.ll[:, 0:1], MID, "ll0")
     ts(T.ee[:], T.cp[:], pcol, None, A.is_equal, None, ["cp", "rp"], ["ee"], 0.16)
     ts(T.eq[:], T.nn[:, 0:8], 256.0, rcol, A.add, A.is_equal, ["nn", "rp"], ["eq"])
     ts(T.lt[:], T.nn[:, 0:8], 256.0, rcol, A.add, A.is_gt, ["nn", "rp"], ["lt"])
-    ts(wcol, rcol, 16.0, 15.0, A.mult, A.add, ["rp"], ["wcol"])
-    ts(ecol, rcol, 128.0, pcol, A.mult, A.add, ["rp"], ["ecol"])
-    ts(mcol, pcol, 8.0, None, A.is_equal, None, ["rp"], ["mcol"])
-    ts(T.z8[:], T.nn[:, 0:8], 512.0, 256.0 * 512 + 256, A.mult, A.add, ["nn"], ["z8"])
     for b in range(8):
         act(T.sel[:, 128 * b:128 * b + 128], T.ee[:], F.Identity, ["ee", "eq"], ["sel%d" % b], 0.16, scale=T.eq[:, b:b + 1])
+    ts(wcol, rcol, 16.0, 15.0, A.mult, A.add, ["rp"], ["wcol"])
+    ts(mcol, pcol, 0.0, None, A.is_equal, None, ["rp"], ["mcol"])
+    ts(ocol, rcol, float(8 * me), -MID, A.add, A.mult, ["rp"], ["ocol"])
+    tt(lecol, T.lt[:, me:me + 1], T.eq[:, me:me + 1], A.add, ["lt", "eq"], ["lecol"])
     ts(T.uu[:], T.lt[:], 16777216.0, None, A.mult, None, ["lt"], ["uu"])
-    ts(T.mc[:], T.z8[:], mcol, None, A.mult, None, ["z8", "mcol"], ["mc"])
-    for c0, c1 in ((0, 512), (512, 1024), (1024, 1152)):
-        ts(T.we[:, c0:c1], T.nn[:, 0:c1 - c0], float(256 + c0 - 112), ecol, A.add, A.is_equal, ["nn", "ecol"], ["we%d" % c0], U / 2)
     ts(T.wd[:], T.nn[:, 0:144], 256.0, wcol, A.add, A.is_equal, ["nn", "wcol"], ["wd"])
     tt(T.uu[:], T.uu[:], T.eq[:], A.add, ["eq"], ["uu"])
-    ts(T.ni[:], T.nn[:, 0:128], acol, -1.0, A.is_equal, A.mult, ["nn", "acol"], ["ni"])
-    ts(T.ibig[:], T.nn[:, 0:128], acol, float(2 ** 41), A.is_equal, A.mult, ["nn", "acol"], ["ibig"])
-    ts(T.nib[:], T.nn[:, 0:128], acol, -float(2 ** 20), A.is_equal, A.mult, ["nn", "acol"], ["nib"])
-    ts(T.blk512[:], T.cb[:], rcol, 512.0, A.is_equal, A.mult, ["cb", "rp"], ["blk512"], 0.16)
+    for name, v in (("ni", -1.0), ("nk", -1024.0), ("ng", -2.0 ** 32), ("old", 2.0 ** 43), ("dgo", ocol)):
+        ts(T[name][:], T.nn[:, 0:128], acol, v, A.is_equal, A.mult, ["nn", "acol", "ocol"], [name])
+    ts(T.pb0[:], T.cb[:], rcol, mcol, A.is_equal, A.mult, ["cb", "rp", "mcol"], ["pb0"], 0.16)
+    for name, v in (("pk", 1024.0), ("pg", 2.0 ** 32)):
+        ts(T[name][:], T.pb0[:], v, None, A.mult, None, ["pb0"], [name])
     ts(T.blk16[:], T.cb[:], rcol, 16.0, A.is_equal, A.mult, ["cb", "rp"], ["blk16"], 0.16)
     ts(T.tmpc[:], T.cb[:], rcol, None, A.is_gt, None, ["cb", "rp"], ["tmpc"], 0.16)
     tt(T.e2[:], T.tmpc[:], T.ee[:], A.mult, ["tmpc", "ee"], ["e2"], 0.3)
+    act(T.wb[:, 0:128], T.ee[:], F.Identity, ["ee", "lt"], ["wb0"], 0.16, scale=T.lt[:, me:me + 1])
+    act(T.wb[:, 128:256], T.ee[:], F.Identity, ["ee", "lecol"], ["wb1"], 0.16, scale=lecol)
     MW = ["mw%d" % b for b in range(8)]
-    for b in range(8):
-        o, col = T.mwin[:, 512 * b:512 * b + 512], T.mc[:, b:b + 1]
-        op({"V": (f_ts(o, T.nn[:], 0.0, col, A.mult, A.add), U / 2), "S": (f_act(o, T.zero[:], F.Identity, bias=col), U)}, ["nn", "zero", "mc"], [MW[b]])
+    for o, key in [(T.mwin[:, 512 * b:512 * b + 512], MW[b]) for b in range(8)] + [(T[k][:], k) for k in ("cc", "j1", "jn")]:
+        op({"V": (f_ts(o, T.nn[:], 0.0, None, A.mult, None), U / 2), "S": (f_act(o, T.zero[:], F.Copy), U)}, ["nn", "zero"], [key])
+    later[0] = 100
     vcopy(T.rchf[:], T.rchi[:], ["rchi"], ["rchf"])
-    ts(T.nrch[:], T.rchi[:], -1.0, None, A.mult, None, ["rchi"], ["nrch"])
+    ts(T.scl[:], T.rchi[:], 0.5, None, A.add, None, ["rchi"], ["scl"])
+    op({"V": (lambda: g.vector.reciprocal(T.rec[:], T.scl[:]), 0.3)}, ["scl"], ["rec"])
+    ts(T.rec[:], T.rec[:], TURN, None, A.mult, None, [], ["rec"])
+    ts(T.steps[:], T.nn[:, 0:16], 248.0, 2.0 ** -24, A.add, A.mult, ["nn"], ["steps"])
+    for k in range(16):
+        c0 = T.rec[:, k:k + 1]
+        act(T.cand[:, k, :], T.steps[:], F.Identity, ["steps", "rec"], ["cand%d" % k], scale=c0, bias=c0)
+    for k in range(16):
+        act(T.fits[:, k, :], T.cand[:, k, :], F.Abs, ["cand%d" % k, "rchf"], ["fits%d" % k], scale=T.rchf[:, k:k + 1])
+    ts(T.fits[:], T.fits[:], TURN, None, A.is_le, None, ["fits%d" % k for k in range(16)], ["fits"], U / 2)
+    tt(T.cand[:], T.cand[:], T.fits[:], A.mult, ["fits"], ["cand%d" % k for k in range(16)] + ["cand"], U)
+    for w in (8, 4, 2):
+        tt(T.cand[:, :, 0:w], T.cand[:, :, 0:w], T.cand[:, :, w:2 * w], A.max, [], ["cand"], U * w / 16)
+    tt(T.scl[:], T.cand[:, :, 0], T.cand[:, :, 1], A.max, ["cand"], ["scl"])
+    vcopy(T.cdu[:], T.cdi[:], ["cdi"], ["cdu"])
+    later[0] = 0
 
-    TB = ["pt0", "pt1", "pt2", "pt3", "pf", "pm", "pt0", "pt1"]
     BW = ["bw%d" % b for b in range(8)]
 
-    def table_mm(blocks, part):
-        for b in blocks:
-            mm(T[TB[b]][:], T.sel[:, 128 * b:128 * b + 128], T[part][:], part == "hi", part == "lo", ["sel%d" % b, part],
-               [TB[b]] + (["table"] if b == 7 else []))
-
-    def table_copy():
+    def table(banks):
+        def part(b, j):
+            mm(T[banks[b]][:], T.sel[:, 128 * b:128 * b + 128], T[("hc", "lc")[j]][:], j == 0, j == 1, ["sel%d" % b, ("hc", "lc")[j]], [banks[b]])
+        for j in range(2):
+            for b in range(8):
+                if banks[b] not in banks[:b]:
+                    part(b, j)
         for b in range(8):
-            shift(T.bwin[:, 512 * b:512 * b + 512], T[TB[b]][:], T.bias[:, b:b + 1], ["bias"], [TB[b], BW[b]], U)
-            if b < 2:
-                table_mm([6 + b], "hi")
-                table_mm([6 + b], "lo")
+            shift(T.bwin[:, 512 * b:512 * b + 512], T[banks[b]][:], T.bias[:, b:b + 1], ["bias"], [banks[b], BW[b]], U)
+            for again in range(b + 1, 8):
+                if banks[again] == banks[b]:
+                    part(again, 0)
+                    part(again, 1)
 
-    hot[0] = True
-    for j in range(4):
-        mm(T.pr[:, 128 * j:128 * j + 128], T.ls[:, :, j], T.ib[:], True, True, ["ls", "lsown", "ib"], ["pr"], PU / 4)
-    scan(T.ll[:, 1:513], T.pr[:], T.zero[:], MID, ["zero"], ["pr", "ll"], U)
-    act(T.hi[:], T.ll[:, 0:512], F.Copy, ["ll", "ll0"], ["hi"], U)
+    for bank in ("pm", "pr"):
+        for j in range(4):
+            mm(T[bank][:, 128 * j:128 * j + 128], T.ls[:, :, j], T.ib[:], True, True, ["ls", "lsown", "ib"], [bank], PU / 4)
+    act(T.szr[:], T.pm[:], F.Copy, [], ["pm", "szr"], U)
     tt(T.x8[:], T.ls[:, 0::16, 4], T.ls[:, 1::16, 4], A.add, ["ls", "lsown"], ["x8"])
     scan(T.pre[:, 1:9], T.x8[:], T.zero[:, 0:8], 0.0, ["x8", "zero"], ["pre"])
     ts(T.z8[:], T.x8[:], T.lt[:, me:me + 1], None, A.mult, None, ["x8", "lt"], ["z8"])
     mm(T.pn[:, 0:8], T.ee[:], T.pre[:, 0:8], True, False, ["ee", "pre", "pre0"], ["pn"], PU / 2)
     mm(T.pn[:, 0:8], T.ee[:], T.z8[:], False, True, ["ee", "z8"], ["pn"], PU / 2)
-    tt(T.lo[:], T.ll[:, 0:512], T.hi[:], A.subtract, ["ll", "ll0", "hi"], ["lo"], 2 * U)
-    table_mm(range(6), "hi")
-    table_mm(range(6), "lo")
+    scan(T.ll[:, 1:512], T.pr[:, 0:511], T.zero[:, 0:511], MID, ["zero"], ["pr", "ll"], U)
     tt(T.x8[:], T.pn[:, 0:8], T.eq[:], A.mult, ["eq"], ["pn", "x8"])
     total(T.own[:, 0:1], T.x8[:], ["x8"], ["own"])
-    ts(T.bias[:], T.pn[:, 0:8], T.own[:, 0:1], None, A.subtract, None, ["own"], ["pn", "bias"])
-    table_copy()
-    for e in range(8):
-        for r in range(8):
-            c0 = 128 * e + 112 - 16 * r
-            mm(T.pn[:, e::8], T.we[:, c0:c0 + 128], T.lr[:, 64 * r:64 * r + 64], r == 0, r == 7, ["we0", "we512", "we1024", "lr", "lrown"], ["pn"], PU / 8)
-    ts(T.lst[:], T.pn[:], 2048.0, None, A.add, None, [], ["pn", "lst"], U)
-    hot[0] = False
-    copy(T.szr[:], T.pr[:], [], ["pr", "szr"], U)
-    for j in range(4):
-        mm(T.pr[:, 128 * j:128 * j + 128], T.lr[:, j::4], T.ih[:], True, True, ["lr", "lrown", "ih"], ["pr"], PU / 4)
-    vcopy(T.cdu[:], T.cdi[:], ["cdi"], ["cdu"])
-    act(T.cc[:], T.nn[:, 0:512].indirect(T.cdu[:, 0:32]), F.Copy, ["nn", "cdu"], ["cc"], GU)
+    ts(T.bias[:], T.pn[:, 0:8], T.own[:, 0:1], MID, A.subtract, A.add, ["own"], ["pn", "bias"])
+    act(T.bwin[:, 0::512], T.bias[:], F.Copy, ["bias"], ["bw"])
+    for b, bank in enumerate(["pf", "pt0", "pt1", "pt2", "pt3", "pm", "pf", "pt0"]):
+        mm(T[bank][:], T.sel[:, 128 * b:128 * b + 128], T.szr[:], True, True, ["sel%d" % b, "szr"], [bank])
+        scan(T.bwin[:, 512 * b + 1:512 * b + 512], T[bank][:, 0:511], T.zero[:, 0:511], T.bias[:, b:b + 1], ["zero", "bias"], [bank, BW[b]], U)
 
-    def len_first(sz, dead, bank):
-        mm(T[bank][:], T.ib[:], T[sz][:], True, False, ["ib", sz], [bank])
-        mm(T[bank][:], T.ni[:], T[dead][:], False, False, ["ni", dead], [bank])
-
-    def len_last(far, out, bank, kw):
-        mm(T[bank][:], T.blk16[:], T[far][:], False, True, ["blk16", far], [bank])
-        act(T[out][:], T[bank][:], F.Relu, [], [bank, out] + (["totown"] if kw else []), U, **kw)
-
-    def deadw(j, out, bank):
-        mm(T[bank][:], T.ib[:], T[j][:], True, False, ["ib", j], [bank])
-        mm(T[bank][:], T.ni[:], T.nn[:], False, True, ["ni", "nn"], [bank])
-        act(T[out][:], T[bank][:], F.Relu, [], [bank, out], U, scale=-1024.0)
-
-    for t in range(1, RO + 1):
-        last = t == RO
-        src_m = "jj" if t == 1 else "mm"
-        if t > 1:
-            mm(T.pf[:], T.ibig[:], T.far[:], True, False, ["ibig", "far"], ["pf"])
-            mm(T.pf[:], T.nib[:], T.dead[:], False, False, ["nib", "dead"], ["pf"])
-
-        act(T.rr[:], T.pr[:], F.Identity, [], ["pr", "rr"], U, bias=2048.0 if t == 1 else 0.0)
-        if last:
-            dmas("Y", "str", [(T.sr[:], T.rr[:])], ["rr"], ["sr"])
-            dmas("Y", "rown", [(T.dr[me], T.rr[mine, :])], ["rr"], ["drown"])
-            send("ro", lambda r: T.sr[r], T.dr[me], ["sr"], "dr", PLAN["big"])
-        dmas("Y", "r%d" % t, [(T.r2[:], T.rr[:])], ["rr"], ["r2"])
-        tt(T.neq[:], T.rr[:, 0:512].indirect(T.cdu[:, 0:32]), T.r2[:], A.not_equal, ["rr", "r2", "cdu"], ["neq"], GU)
-        mm(T.pm[:], T.ib[:], T.cc[:], True, False, ["ib", "cc"], ["pm"])
-        mm(T.pm[:], T.blk512[:], T.neq[:], False, True, ["blk512", "neq"], ["pm"])
-        tt(T.jj[:], T.pm[:], T.nn[:], A.min, ["nn"], ["pm", "jj"], U)
-        if last:
-            dmas("Y", "stj", [(T.sj[:], T.jj[:])], ["jj"], ["sj"])
-            dmas("Y", "jown", [(T.dj[me], T.jj[mine, :])], ["jj"], ["djown"])
-            send("jo", lambda r: T.sj[r], T.dj[me], ["sj"], "dj", PLAN["big"])
-            dmas("Y", "yr", [(T.yr[:], T.dr[:])], ["dr", "drown"], [])
-            dmas("Y", "ljn", [(T.jn[:], T.dj[:])], ["dj", "djown"], ["jn"])
-            dmas("Y", "lj8", [(T.j8[0:8, :], T.dj[:, 0:8, :])], ["dj", "djown"], ["j8"])
+    def folds(t):
+        if t == 1:
+            m = "j1"
+            dmas("Y", "mw1", [(T.mwin[16 * r:16 * r + 1, :], T.dc[:, 0:64, :]) for r in range(8)], ["dc", "dcown"], MW)
+            dmas("Y", "lj1", [(T.j1[0::16, :], T.dc[:, 0:64, :])], ["dc", "dcown"], ["j1"])
+            dmas("Y", "lcc", [(T.cc[0::16, :], T.dc[:, 64:128, :])], ["dc", "dcown"], ["cc"])
         else:
-            if t > 1:
-                act(T.mm[:], T.jj[:, 0:512].indirect(T.ml[:, 32 * (t - 2):32 * (t - 1)]), F.Copy, ["jj", "ml%d" % t], ["mm"], GU)
-            dmas("Y", "mw%d" % t, [(T.mwin[p::16, 512 * p:512 * p + 512], T[src_m][16 * p:16 * p + 8, :]) for p in range(8)], [src_m], MW)
-            for p in range(16):
-                mm(T.pn[:, 0:32], T.wd[:, 15 - p:143 - p], T[src_m][:, p::16], p == 0, p == 15, ["wd", src_m], ["pn"], PU / 8)
-            ts(T.ml[:, 32 * (t - 1):32 * t], T.pn[:, 0:32], 0.0625, 256.0, A.mult, A.add, [], ["pn", "ml%d" % (t + 1)])
-        deadw("jj", "dead", "pm")
-        len_first("szr", "dead", "pm")
-
-        dmas("Y", "l%d" % t, [(T.l2[:, 512 * j:512 * j + 512], T.ll[:, 0:512]) for j in range(2)], ["ll", "ll0"], ["l2"])
-
-        def gather(k, n):
-            tt(T.dd[:, 512 * k:512 * (k + n)], T.bwin[:, 0:4096].indirect(T.lst[:, 32 * k:32 * (k + n)]), T.l2[:, 0:512 * n], A.subtract,
-               BW + ["lst", "l2"], ["dd%d" % (k + j) for j in range(n)], n * GU - (n - 1) * 0.06)
-
-        def absol(k, n):
-            d = T.dd[:, 512 * k:512 * (k + n)]
-            act(d, d, F.Abs, [], ["dd%d" % (k + j) for j in range(n)], n * U)
-
-        def compare(k):
-            o, d = T.ind[:, 512 * k:512 * k + 512], T.dd[:, 512 * k:512 * k + 512]
-            op({"V": (f_ts(o, d, T.rchf[:, k:k + 1], None, A.is_gt, None), U), "S": (f_act(o, d, F.Relu, bias=T.nrch[:, k:k + 1]), U)},
-               ["dd%d" % k, "rchf", "nrch"], ["ind%d" % k])
-            mm(T.pf[:], T.wd[:, 15 - k:143 - k], o, t == 1 and k == 0, k == 15, ["wd", "ind%d" % k], ["pf"])
-
-        for q in range(8 + PLAN["lag"]):
-            hot[0] = q >= 7
-            if q in (0, 7):
-                for k in (2 * q, 2 * q + 1):
-                    gather(k, 1)
-                    absol(k, 1)
-            elif q < 7:
-                gather(2 * q, 2)
-                absol(2 * q, 2)
-            if q >= PLAN["lag"]:
-                compare(2 * (q - PLAN["lag"]))
-                compare(2 * (q - PLAN["lag"]) + 1)
-
-        hot[0] = True
-        ts(T.far[:], T.pf[:], 0.0, None, A.is_gt, None, [], ["pf", "far"], U)
-        if not last:
-            slot = (8 * (t - 1) + me) * 4
-            tcol = T.tot[:, slot:slot + 1]
-            lists_t = T.ml[:, 32 * (t - 1):32 * t]
-            len_last("far", "ln", "pm", {"accum_out": tcol})
-            send("t%d" % t, lambda r: tcol, tcol, ["totown"], "tot%d" % t, PLAN["msg"])
-            scan(T.ll[:, 1:513], T.ln[:], T.zero[:], MID, ["ln", "zero"], ["ll"], U)
-            act(T.hi[:], T.ll[:, 0:512].indirect(lists_t), F.Copy, ["ll", "ll0", "ml%d" % (t + 1)], ["hi"], GU)
-            tt(T.lo[:], T.ll[:, 0:512].indirect(lists_t), T.hi[:], A.subtract, ["ll", "ll0", "hi", "ml%d" % (t + 1)], ["lo"], GU)
-            scan(T.pre[:, 1:9], T.tot[:, 32 * (t - 1):32 * t:4], T.zero[:, 0:8], 0.0, ["tot%d" % t, "totown", "zero"], ["pre"])
-            mm(T.pn[:, 8:9], T.e2[:], T.pre[:, 8:9], True, True, ["e2", "pre"], ["pn"], PU / 2)
-            if me == 0:
-                ts(T.z8[:], T.lt[:], T.pre[:, 8:9], None, A.mult, None, ["lt", "pre"], ["z8"])
+            m = "mm"
+            if PLAN["neq"] == "V":
+                tt(T.neq[:], T.rl[:, 0:512].indirect(T.cdu[:, 0:32]), T.rl2[:], A.not_equal, ["rl", "rl2", "cdu"], ["neq"], GU)
             else:
-                ts(T.z8[:], T.uu[:], T.pre[:, me:me + 1], T.pre[:, 8:9], A.mult, A.min, ["uu", "pre"], ["z8"])
-            mm(T.pn[:, 0:8], T.ee[:], T.z8[:], True, True, ["ee", "z8"], ["pn"], PU / 2)
-            ts(T.bias[:], T.pn[:, 0:8], T.pn[:, 8:9], T.pre[:, me:me + 1], A.subtract, A.subtract, ["pre", "pre0"], ["pn", "bias"])
-            table_mm(range(6), "hi")
-            table_mm(range(6), "lo")
-            table_copy()
-            hot[0] = False
-            for k in range(16):
-                o = T.gr[:, 512 * k:512 * k + 512]
-                src = T.mwin[:, 0:4096].indirect(T.lst[:, 32 * k:32 * k + 32])
-                if k < PLAN["both"]:
-                    copy(o, src, MW + ["lst"], ["gr%d" % k], GU)
-                else:
-                    act(o, src, F.Copy, MW + ["lst"], ["gr%d" % k], GU)
-                mm(T.pr[:], T.wd[:, 15 - k:143 - k], o, k == 0, k == 15, ["wd", "gr%d" % k] + (["table"] if k >= PLAN["early"] else []), ["pr"])
+                act(T.rl2[:], T.rl[:, 0:512].indirect(T.cdu[:, 0:32]), F.Copy, ["rl", "cdu"], ["rl2"], GU)
+                sums("pr", [("ni", "rl"), ("ib", "rl2")])
+                act(T.neq[:], T.pr[:], F.Abs, [], ["pr", "neq"], U)
+            sums("pr", [("pb0", "cc"), ("blk512", "neq")])
+            tt(T.jj[:], T.pr[:], T.nn[:], A.min, ["nn"], ["pr", "jj"], U)
+            if t < RO:
+                copy(T.mm[:], T.jj[:, 0:512].indirect(T.ml[:, 32 * (t - 2):32 * (t - 1)]), ["jj", "ml%d" % t], ["mm"], GU)
+                dmas("Y", "mw%d" % t, [(T.mwin[0::16, 512 * p:512 * p + 512], T.mm[16 * p:16 * p + 8, :]) for p in range(8)], ["mm"], MW)
+        if t < RO:
+            for p in range(16):
+                mm(T.pr[:, 0:32], T.wd[:, 15 - p:143 - p], T[m][:, p::16], p == 0, p == 15, ["wd", m], ["pr"], PU / 8)
+            ts(T.ml[:, 32 * (t - 1):32 * t], T.pr[:, 0:32], 1.0 if t == 1 else 0.0625, 256.0, A.mult, A.add, [], ["pr", "ml%d" % (t + 1)])
+
+    def home():
+        dmas("Y", "str", [(T.sr[:], T.rl[:])], ["rl"], ["sr"])
+        dmas("Y", "rown", [(T.dr[me], T.rl[mine, :])], ["rl"], ["drown"])
+        dmas("Y", "stj", [(T.sj[:], T.jj[0::16, :])], ["jj"], ["sj"])
+        dmas("Y", "jown", [(T.dj[me], T.jj[16 * me:16 * me + 1, :])], ["jj"], ["djown"])
+        send("ro", lambda r: T.sr[r], T.dr[me], ["sr", "tot3"], "dr", PLAN["big"])
+        send("jo", lambda r: T.sj[r], T.dj[me], ["sj"], "dj", PLAN["msg"])
+        dmas("Y", "ljn", [(T.jn[0::16, :], T.dj[:])], ["dj", "djown"], ["jn"])
+        dmas("Y", "lj8", [(T.j8[0:8, :], T.dj[:])], ["dj", "djown"], ["j8"])
+        dmas("Y", "lrn", [(T.rn[:], T.dr[:])], ["dr", "drown"], ["rn"])
+        for j in range(4):
+            mm(T.pt1[:, j::4], T.jj[:, 128 * j:128 * j + 128], T.ib[:], True, False, ["jj", "ib"], ["pt1"], PU / 4)
+            mm(T.pt1[:, j::4], T.nn[:, 128 * j:128 * j + 128], T.ni[:], False, True, ["nn", "ni"], ["pt1"], PU / 4)
+        ts(T.alv[:], T.pt1[:], 0.0, 1.0, A.is_equal, A.add, [], ["pt1", "alv"], U)
+
+    def renames(t):
+        k = 0
+        for n in RENAMES:
+            copy(T.gr[:, 512 * k:512 * (k + n)], T.mwin[:, 0:4096].indirect(T.lst[:, 32 * k:32 * (k + n)]), MW + ["lst"],
+                 ["gr%d" % (k + j) for j in range(n)], many(n))
+            k += n
+        for name, out in (("r", "rl"), ("q", "rl2"))[:2 if PLAN["neq"] == "V" else 1]:
+            dmas("Y", name + str(t), [(T[out][:], T.gr[0::16, :])], ["gr%d" % j for j in range(16)], [out])
+
+    def marks(t):
+        def over(k):
+            o = T.ind[:, 512 * k:512 * k + 512]
+            i = op({"V": (f_ts(o, o, EDGE, None, A.is_gt, None), U / 2 + 0.03), "S": (f_act(o, o, F.Relu, bias=-EDGE), U)}, [], ["ind%d" % k])
+            calls[i]["first"] = OVER[t - 1][k]
+            mm(T.pf[:], T.wd[:, 15 - k:143 - k], o, k == 0 and t == 1, k == 15, ["wd", "ind%d" % k], ["pf"])
+
+        dmas("Y", "l%d" % t, [(T.ll[:, 512:1024], T.ll[:, 0:512])], ["ll", "ll0"], ["l2"])
+        k = 0
+        for n in GATHERS:
+            tt(T.dd[:, 512 * k:512 * (k + n)], T.bwin[:, 0:4096].indirect(T.lst[:, 32 * k:32 * (k + n)]), T.ll[:, 0:512 * n], A.subtract,
+               BW + ["bw", "lst", "ll", "ll0"] + ["l2"] * (n - 1), ["dd%d" % (k + j) for j in range(n)], many(n))
+            for j in range(k, k + n):
+                act(T.ind[:, 512 * j:512 * j + 512], T.dd[:, 512 * j:512 * j + 512], F.Abs, ["dd%d" % j, "scl"], ["ind%d" % j], U, scale=T.scl[:, j:j + 1])
+                if j >= PLAN["lag"]:
+                    over(j - PLAN["lag"])
+            k += n
+        for j in range(16 - PLAN["lag"], 16):
+            over(j)
+
+    folds(1)
+    for t in range(1, RO + 1):
+        if t > 1:
+            sums("pf", [("pg", "j1" if t == 2 else "jj"), ("ng", "nn"), ("old", "far")], sp=False)
+            renames(t)
+            folds(t)
+        if t == RO:
+            home()
+        marks(t)
+        sums("pm", [("pk", "j1" if t == 1 else "jj"), ("nk", "nn"), ("ib", "szr")], sp=False)
+        ts(T.far[:], T.pf[:], 0.0, None, A.is_gt, None, [], ["pf", "far"], U)
+        tcol = T.tot[:, (8 * (t - 1) + me) * 4:(8 * (t - 1) + me) * 4 + 1] if t < RO else T.tot0[:, 4:5]
+        sums("pm", [("blk16", "far")], st=False)
+        act(T.ln[:], T.pm[:], F.Relu, [], ["pm", "ln", "totown"], U, accum_out=tcol)
+        if t == RO:
+            break
+        lists_t = T.ml[:, 32 * (t - 1):32 * t]
+        send("t%d" % t, lambda r: tcol, tcol, ["totown"], "tot%d" % t, PLAN["msg"])
+        scan(T.ll[:, 1:512], T.ln[:, 0:511], T.zero[:, 0:511], MID, ["ln", "zero"], ["ll"], U)
+        copy(T.hc[:], T.ll[:, 0:512].indirect(lists_t), ["ll", "ll0", "ml%d" % (t + 1)], ["hc"], GU)
+        tt(T.lc[:], T.ll[:, 0:512].indirect(lists_t), T.hc[:], A.subtract, ["ll", "ll0", "hc", "ml%d" % (t + 1)], ["lc"], GU)
+        scan(T.pre[:, 1:9], T.tot[:, 32 * (t - 1):32 * t:4], T.zero[:, 0:8], 0.0, ["tot%d" % t, "totown", "zero"], ["pre"])
+        mm(T.pn[:, 8:9], T.e2[:], T.pre[:, 8:9], True, True, ["e2", "pre"], ["pn"], PU / 2)
+        if me == 0:
+            ts(T.z8[:], T.lt[:], T.pre[:, 8:9], None, A.mult, None, ["uu", "pre"], ["z8"])
         else:
-            tcol = T.tot0[:, 4:5]
-            len_last("far", "ln", "pm", {"accum_out": tcol})
-            for j in range(4):
-                mm(T.pt0[:, j::4], T.far[:, 128 * j:128 * j + 128], T.ib[:], True, True, ["far", "ib"], ["pt0"], PU / 4)
-            vcopy(T.ft[:, :, 0:4], T.pt0[:], [], ["pt0", "ft"], U)
-            ts(T.ft[:, 0::2, 4], T.zero[:, 0:64], tcol, MID, A.add, A.add, ["zero", "totown"], ["fthi"])
-            ts(T.own[:, 2:3], tcol, MID, None, A.add, None, ["totown"], ["own2"])
-            ts(T.ft[:, 1::2, 4], T.ft[:, 0::2, 4], -1.0, T.own[:, 2:3], A.mult, A.add, ["fthi", "own2"], ["ftlo"])
-            send("fo", lambda r: T.ft[:, 16 * r:16 * r + 16, :], T.lf[:, mine, :], ["ft", "fthi", "ftlo"], "lf", PLAN["msg"] + 1.0)
-            vcopy(T.lf[:, mine, :], T.ft[:, mine, :], ["ft", "fthi", "ftlo"], ["lfown"])
-            mm(T.pn[:], T.ib[:], T.jn[:], True, False, ["ib", "jn", "ft"], ["pn"])
-            mm(T.pn[:], T.ni[:], T.nn[:], False, True, ["ni", "nn"], ["pn"])
-            act(T.deadn[:], T.pn[:], F.Relu, [], ["pn", "deadn"], U, scale=-1024.0)
-            act(T.j8f[0:8, :], T.j8[0:8, :], F.Identity, ["j8", "deadn"], ["j8f"], U, bias=float(256 + S * me))
-            dmas("Y", "yj", [(T.yj[:], T.j8f[0:8, :])], ["j8f"], [])
-            len_first("szb", "deadn", "pt3")
-            for p in ("pt1", "pt2"):
-                for j in range(4):
-                    mm(T[p][:, 128 * j:128 * j + 128], T.lf[:, :, j], T.ib[:], True, True, ["lf", "lfown", "ib"], [p], PU / 4)
-            act(T.farn[:], T.pt1[:], F.Copy, [], ["pt1", "farn"], U)
-            tt(T.x8[:], T.lf[:, 0::16, 4], T.lf[:, 1::16, 4], A.add, ["lf", "lfown"], ["x8"])
-            scan(T.pre[:, 1:9], T.x8[:], T.mid8[:], 0.0, ["x8", "mid8"], ["pre"])
-            ts(T.own[:, 1:2], T.pre[:, 8:9], T.lt[:, me:me + 1], None, A.mult, None, ["pre", "lt"], ["own1"])
-            ts(T.z8[:], T.pre[:, 0:8], T.eq[:, me:me + 1], T.own[:, 1:2], A.mult, A.add, ["pre", "pre0", "eq", "own1"], ["z8"])
-            mm(T.pn[:, 0:8], T.ee[:], T.z8[:], True, True, ["ee", "z8"], ["pn"], PU / 2)
-            len_last("farn", "lnn", "pt3", {})
-            tt(T.x8[:], T.pn[:, 0:8], T.eq[:], A.mult, ["eq"], ["pn", "x8"])
-            total(T.la[:, 0:1], T.x8[:], ["x8"], ["la0"])
-            scan(T.la[:, 1:512], T.lnn[:, 0:511], T.zero[:, 0:511], T.la[:, 0:1], ["lnn", "la0", "zero"], ["la"], U)
-            dmas("Y", "ya", [(T.ya[:], T.la[:, 0:512])], ["la", "la0"], [])
-            vcopy(T.yfb[:], T.pt2[:], [], ["pt2", "yfb"], U)
-            dmas("S", "yf", [(T.yf[:], T.yfb[:])], ["yfb"], [])
+            ts(T.z8[:], T.uu[:], T.pre[:, me:me + 1], T.pre[:, 8:9], A.mult, A.min, ["uu", "pre"], ["z8"])
+        mm(T.pn[:, 0:8], T.ee[:], T.z8[:], True, True, ["ee", "z8"], ["pn"], PU / 2)
+        ts(T.bias[:], T.pn[:, 0:8], T.pn[:, 8:9], T.pre[:, me:me + 1], A.subtract, A.subtract, ["pre", "pre0"], ["pn", "bias"])
+        table(["pf", "pt0", "pt1", "pt2", "pt3", "pm", "pf", "pt0"])
+
+    for j in range(4):
+        mm(T.pt0[:, j::4], T.far[:, 128 * j:128 * j + 128], T.ib[:], True, True, ["far", "ib"], ["pt0"], PU / 4)
+    tt(T.ft[:, :, 0:4], T.pt0[:], T.alv[:], A.mult, ["alv"], ["pt0", "ft"], U)
+    ts(T.ft[:, 0::2, 4], T.zero[:, 0:64], tcol, MID, A.add, A.add, ["zero", "totown"], ["fthi"])
+    ts(T.own[:, 2:3], tcol, MID, None, A.add, None, ["totown"], ["own2"])
+    ts(T.ft[:, 1::2, 4], T.ft[:, 0::2, 4], -1.0, T.own[:, 2:3], A.mult, A.add, ["fthi", "own2"], ["ftlo"])
+    send("fo", lambda r: T.ft[:, 16 * r:16 * r + 16, :], T.lf[:, mine, :], ["ft", "fthi", "ftlo"], "lf", PLAN["msg"] + 1.0)
+    vcopy(T.lf[:, mine, :], T.ft[:, mine, :], ["ft", "fthi", "ftlo"], ["lfown"])
+    sums("pr", [("ib", "rko"), ("ib", "rn")])
+    shift(T.rr[:], T.pr[:], 256.0 - LIFT, [], ["pr", "rr"], U)
+    dmas("Y", "yr", [(T.yr[:], T.rr[:])], ["rr"], [])
+    sums("pr", [("pk", "jn"), ("nk", "nn"), ("ib", "szb")])
+    act(T.sza[:], T.pr[:], F.Relu, [], ["pr", "sza"], U)
+    shift(T.j8f[0:8, :], T.j8[0:8, :], float(256 + S * me), ["j8"], ["j8f"], U)
+    dmas("Y", "yj", [(T.yj[:], T.j8f[0:8, :])], ["j8f"], [])
+    sums("pt3", [("ib", "sza")], sp=False)
+    mm(T.pn[:, 0:1], T.dgo[:], T.one[:, 0:1], True, False, ["dgo", "one"], ["pn"], PU / 8)
+    for j in range(4):
+        mm(T.pt1[:, 128 * j:128 * j + 128], T.lf[:, :, j], T.ib[:], True, True, ["lf", "lfown", "ib"], ["pt1"], PU / 4)
+    act(T.farn[:], T.pt1[:], F.Relu, [], ["pt1", "farn"], U, bias=-1.0)
+    for b in range(16):
+        c0 = 112 - 16 * (b // 2)
+        mm(T.pn[:, 0:1], T.wb[:, c0:c0 + 128], T.lf[:, 16 * (b // 2) + b % 2, 4:5], False, b == 15, ["wb0", "wb1", "lf", "lfown"], ["pn"], PU / 8)
+    sums("pt3", [("blk16", "farn")], st=False)
+    for j in range(4):
+        mm(T.pt2[:, 128 * j:128 * j + 128], T.lf[:, :, j], T.ib[:], True, True, ["lf", "lfown", "ib"], ["pt2"], PU / 4)
+    vcopy(T.la[:, 0:1], T.pn[:, 0:1], [], ["pn", "la0"])
+    scan(T.la[:, 1:512], T.pt3[:, 0:511], T.zero[:, 0:511], T.la[:, 0:1], ["la0", "zero"], ["pt3", "la"], U)
+    dmas("Y", "ya", [(T.ya[:], T.la[:, 0:512])], ["la", "la0"], [])
+    act(T.yfb[:], T.pt2[:], F.Sign, [], ["pt2", "yfb"], U)
+    dmas("S", "yf", [(T.yf[:], T.yfb[:])], ["yfb"], [])
 
     count = {"V": 0, "S": 0, "P": 0, "G": 0}
     seen = {q: {} for q in Q}
     token, most = {}, {}
-    for i, q in place(calls):
+    if not ORDER:
+        ORDER.extend(place(calls))
+    for i, q in ORDER:
         c = calls[i]
         if q != "-":
             want = {}

from concourse.bass import DstId, RemoteDMATransfer
from concourse.mybir import AluOpType as A, ActivationFunctionType as F, AxisListType as AX

N, S, RO = 8, 512, 4
MID = -131072.0
LIFT = 98304.0
EDGE = 2.0 - 2.0 ** -6
TURN = 2.0 - 3 * 2.0 ** -8

PLAN = {"U": 0.52, "G": 0.8, "P": 0.35, "s": 0.12, "dma": 2.6, "msg": 3.6, "first": 6.0, "big": 7.0,
        "lag": 3, "neq": "S", "passes": 150, "moves": 4000, "spare": (0.0, 0.2, 0.5, 1.0, 2.0), "shake": 0.5}
CASES = ((1.0, 1.0, 1.0), (0.7, 1.28, 1.0), (1.2, 0.75, 1.0), (0.8, 1.1, 1.4))
GATHERS = (1, 1, 2, 2, 2, 2, 2, 1, 1, 1, 1)
RENAMES = (3, 3, 2, 2, 2, 2, 1, 1)
OVER = ["S" * n + "V" * (16 - n) for n in (7, 5, 5, 7)]

f32, bf, h16, i32, u16 = "float32", "bfloat16", "float16", "int32", "uint16"


def _sb(n, d):
    return ("sbuf", [128, n], d)


SCRATCH = {
    "szi": _sb(512, i32), "rfi": _sb(512, i32), "rfj": _sb(512, i32), "cdo": _sb(32, i32), "cdv": _sb(32, u16),
    "szb": _sb(512, bf), "rfh": _sb(512, h16), "rko": _sb(512, bf), "rkp": _sb(512, bf), "jc": _sb(1024, bf),
    "ms": ("sbuf", [128, 128, 5], bf), "ls": ("sbuf", [128, 128, 5], bf), "mr": ("sbuf", [128, 8, 64], h16), "lso": _sb(512, u16),
    "sh": ("dram", [8, 128, 8], i32), "dh": ("dram", [8, 128, 8], i32), "sc": ("dram", [8, 128, 8], bf), "dc": ("dram", [8, 128, 8], bf),
    "dl": ("dram", [8, 128, 64], u16),
    "cdi": _sb(32, i32), "rchi": _sb(16, i32), "cdu": _sb(32, u16),
    "rl": _sb(512, bf), "rl2": _sb(512, bf), "hc": _sb(512, bf), "lc": _sb(512, bf),
    "nn": _sb(512, bf), "zero": _sb(512, f32), "ai": _sb(4, i32), "col": _sb(16, f32), "one": _sb(8, bf),
    "cb": _sb(128, f32), "cp": _sb(128, f32), "tmpc": _sb(128, f32),
    "ib": _sb(128, bf), "ih": _sb(128, h16), "ni": _sb(128, bf), "nk": _sb(128, bf), "ng": _sb(128, bf), "old": _sb(128, bf),
    "pb0": _sb(128, bf), "pk": _sb(128, bf), "pg": _sb(128, bf), "dgo": _sb(128, bf), "wb": _sb(256, bf),
    "rchf": _sb(16, f32), "rec": _sb(16, f32), "scl": _sb(16, f32), "steps": _sb(16, f32),
    "cand": ("sbuf", [128, 16, 16], f32), "fits": ("sbuf", [128, 16, 16], f32),
    "blk512": _sb(128, bf), "blk16": _sb(128, bf), "ee": _sb(128, f32), "e2": _sb(128, f32),
    "wd": _sb(144, bf), "we": _sb(1152, h16), "sel": _sb(1024, bf),
    "eq": _sb(8, f32), "lt": _sb(8, f32), "uu": _sb(8, f32),
    "tot0": _sb(8, f32), "x8": _sb(8, f32), "z8": _sb(8, f32), "pre": _sb(16, f32), "bias": _sb(8, f32), "own": _sb(8, f32),
    "tot": _sb(96, f32),
    "szr": _sb(512, bf), "ll": _sb(1024, f32), "ln": _sb(512, f32),
    "lst": _sb(512, u16), "ml": _sb(96, u16), "bwin": _sb(4096, f32), "mwin": _sb(4096, bf),
    "dd": _sb(8192, f32), "ind": _sb(8192, bf), "gr": _sb(8192, bf),
    "neq": _sb(512, bf), "cc": _sb(512, bf), "j1": _sb(512, bf), "jj": _sb(512, bf), "mm": _sb(512, bf), "far": _sb(512, bf),
    "sr": ("dram", [8, 128, 64], bf), "dr": ("dram", [8, 128, 64], bf),
    "sj": ("dram", [8, 128, 4], bf), "dj": ("dram", [8, 128, 4], bf),
    "rn": _sb(512, bf), "rr": _sb(512, f32), "jn": _sb(512, bf), "j8": _sb(512, bf), "j8f": _sb(512, f32),
    "alv": _sb(512, bf), "sza": _sb(512, bf), "ft": ("sbuf", [128, 128, 5], bf), "lf": ("sbuf", [128, 128, 5], bf),
    "farn": _sb(512, bf), "yfb": _sb(512, f32), "la": _sb(520, f32),
    "pf": ("psum", [128, 512], f32), "pr": ("psum", [128, 512], f32), "pm": ("psum", [128, 512], f32), "pn": ("psum", [128, 512], f32),
    "pt0": ("psum", [128, 512], f32), "pt1": ("psum", [128, 512], f32), "pt2": ("psum", [128, 512], f32), "pt3": ("psum", [128, 512], f32),
}
_MSG = ["rc", "sz", "rf", "jc", "t1", "t2", "t3", "ro", "jo", "fo"]
_DMA = (["lsz", "lrf", "lrg", "lco", "sth", "stown", "lrc", "lcd", "stc", "cown", "lj1", "lcc", "lown", "lst",
         "str", "rown", "stj", "jown", "lrn", "yr", "ljn", "lj8", "yj", "yf", "ya"]
        + [a + str(t) for a in ("mw", "r", "q", "l") for t in range(1, RO + 1)])
SEMAPHORES = ["V", "S", "P", "G"] + ["a_" + m for m in _MSG] + ["o_" + m for m in _MSG] + ["d_" + d for d in _DMA]


def engine_split(src, cores, topo):
    others = [c for c in cores if c != src]
    off = [c for c in others if topo.chip(c) != topo.chip(src)]
    on = [c for c in others if topo.chip(c) == topo.chip(src)]
    res = {}
    used = []
    for grp in (off, on):
        if not grp:
            continue
        pool = [e for e in topo.engines(src, grp[0]) if e not in used]
        each = 1
        while each * 2 * len(grp) <= len(pool):
            each *= 2
        cnt = [each] * len(grp)
        left = len(pool) - each * len(grp)
        for q in range(len(grp)):
            if left >= each:
                cnt[q] += each
                left -= each
        at = 0
        for c, n in zip(grp, cnt):
            res[c] = pool[at:at + n]
            at += n
        used += pool[:at]
    return res


def place(calls):
    n = len(calls)
    deps = [c["deps"] for c in calls]
    users = [[] for _ in range(n)]
    for i in range(n):
        for d in deps[i]:
            users[d].append(i)

    def time(i, q, case):
        c = calls[i]["alts"][q][1]
        return c * (case[0] if q == "P" else case[1] if q in "VS" and c >= PLAN["G"] else 1.0)

    def sweep(before, after, urgency, back, case, spare):
        start, end, queue = [0.0] * n, [0.0] * n, [None] * n
        busy = {q: [] for q in "VSPGY"}
        left = [len(b) for b in before]
        cand = [i for i in range(n) if left[i] == 0]
        while cand:
            i = min(cand, key=lambda j: urgency[j])
            cand.remove(i)
            best = None
            for q in calls[i].get("first", calls[i]["alts"]):
                t, c = 0.0, time(i, q, case)
                for d in before[i]:
                    later = queue[d] if back else q
                    gap = 0.0 if later == "-" or (q == "P" and queue[d] == "P") else PLAN["s"]
                    t = max(t, end[d] + gap + calls[i if back else d]["lat"] * case[2])
                at = 0
                if q != "-":
                    row = busy[q]
                    at = len(row)
                    while at > 0 and row[at - 1][1] > t:
                        at -= 1
                    while at < len(row) and row[at][0] < t + c - 1e-9:
                        t = max(t, row[at][1])
                        at += 1
                key = t + c + (spare if q == "V" else 0.0)
                if best is None or key < best[0] - 1e-9:
                    best = (key, t + c, t, q, at)
            _, end[i], start[i], queue[i], at = best
            if queue[i] != "-":
                busy[queue[i]].insert(at, (start[i], end[i]))
            for u in after[i]:
                left[u] -= 1
                if left[u] == 0:
                    cand.append(u)
        return start, end, queue

    cost = [{q: [(time(i, q, case), calls[i]["lat"] * case[2]) for case in CASES] for q in calls[i]["alts"]} for i in range(n)]

    def run(order, k):
        end, free, onp, s = [0.0] * n, dict.fromkeys("VSPGY-", 0.0), [False] * n, PLAN["s"]
        last, why = dict.fromkeys("VSPGY-", -1), [None] * n
        for i, q in order:
            t, by, own = (free[q], last[q], True) if q != "-" else (0.0, -1, False)
            onp[i] = q == "P"
            for d in deps[i]:
                e = end[d] if q == "-" or (onp[i] and onp[d]) else end[d] + s
                if e >= t:
                    t, by, own = e, d, False
            c, lat = cost[i][q][k]
            free[q], last[q] = t + c, i
            end[i], why[i] = t + c + lat, (by, own)
        return end, why

    def score(order):
        return sum(max(run(order, k)[0]) for k in range(len(CASES)))

    seed = [1]

    def pick(m):
        seed[0] = (seed[0] * 1103515245 + 12345) % 2 ** 31
        return (seed[0] >> 8) % m

    urgency, best = [c["rank"] for c in calls], None
    for p in range(PLAN["passes"]):
        case, spare = CASES[p // 3 % len(CASES)], PLAN["spare"][p // 3 % len(PLAN["spare"])]
        start, end, queue = sweep(deps, users, urgency, False, case, spare)
        done = [end[i] + calls[i]["lat"] for i in range(n)]
        order = [(i, queue[i]) for i in sorted(range(n), key=lambda j: (start[j], j))]
        if best is None or score(order) < best[0]:
            best = (score(order), order, done)
        if p % 3 == 2:
            done = [e + PLAN["shake"] * pick(1000) / 1000 for e in best[2]]
        urgency = [-e for e in sweep(users, deps, [-e for e in done], True, case, spare)[1]]

    now, order = best[0], best[1]
    for step in range(PLAN["moves"]):
        end, why = run(order, step % len(CASES))
        i, pairs = max(range(n), key=lambda j: end[j]), []
        while i >= 0:
            if why[i][1] and why[i][0] >= 0:
                pairs.append((why[i][0], i))
            i = why[i][0]
        at = {j: p for p, (j, _) in enumerate(order)}
        for _ in range(8):
            (u, v), how = pairs[pick(len(pairs))], pick(4)
            i = v if how % 2 == 0 else u
            q, to = order[at[i]][1], (at[u] - 4 * pick(3), at[v] + 6 * pick(4), at[i] + pick(31) - 15, at[i] + pick(31) - 15)[how]
            if how >= 2:
                q = [o for o in calls[i]["alts"] if o != q or len(calls[i]["alts"]) == 1][0]
            to = min([at[w] - 1 for w in users[i]] + [max([at[d] + 1 for d in deps[i]] + [to, 0])])
            new = order[:at[i]] + order[at[i] + 1:]
            new.insert(to, (i, q))
            tried = score(new)
            if tried <= now:
                now, order = tried, new
                break
    return order


ORDER = []


def rank_program(g, core, T, topo):
    me = T.rank_of(core)
    if me is None:
        return
    cores = list(T.cores)
    Q = {"V": g.vector, "S": g.scalar, "P": g.tensor, "G": g, "Y": g.sync}
    U, GU, PU, SM = PLAN["U"], PLAN["G"], PLAN["P"], 0.07
    split = engine_split(core, cores, topo)
    arrive = sum(len(engine_split(c, cores, topo)[core]) for c in cores if c != core)
    nsent = sum(len(v) for v in split.values())

    calls, writer, readers, later = [], {}, {}, [0]

    def op(alts, rd, wr, lat=0.0, tok=None, more=()):
        deps = set(more)
        for k in rd:
            if k in writer:
                deps.add(writer[k])
        for k in wr:
            if k in writer:
                deps.add(writer[k])
            deps.update(readers.get(k, []))
        i = len(calls)
        calls.append({"alts": alts, "deps": sorted(deps), "lat": lat, "tok": tok, "wr": wr, "rank": i + later[0]})
        for k in rd:
            readers.setdefault(k, []).append(i)
        for k in wr:
            writer[k] = i
            readers[k] = []
        return i

    def dmas(q, name, pairs, rd, wr):
        def emit():
            for o, i in pairs:
                Q[q].dma_start(o, i).then_inc(T.sem["d_" + name], 16)
        op({q: (emit, 0.06 * len(pairs))}, rd, wr, PLAN["dma"], ("d_" + name, 16 * len(pairs)))

    def send(name, src, dst, rd, land, lat):
        tr = []
        for r, c in enumerate(cores):
            if c == core:
                continue
            rid, pid, _ = topo.addr(c)
            m = 0
            for e in split[c]:
                m |= 1 << e
            tr.append(RemoteDMATransfer(dst_ids=[DstId(rid=rid, pnc=pid)], dma_engine_mask=m, remote_sem=T.sem["a_" + name], src=src(r), dst=dst))
        i = op({"G": (lambda: g.remote_dma_fused(tr, local_sem=T.sem["o_" + name]), 0.3)}, rd, ["sends"], 0.0, ("o_" + name, nsent))
        op({"-": (None, 0.0)}, [], [land], lat, ("a_" + name, arrive), [i])

    def f_ts(out, in0, s1, s2, o0, o1):
        if o1 is None:
            return lambda: g.vector.tensor_scalar(out, in0, s1, None, o0)
        return lambda: g.vector.tensor_scalar(out, in0, s1, s2, o0, o1)

    def f_act(out, a, fn, **kw):
        return lambda: g.scalar.activation(out, a, fn, **kw)

    def ts(out, in0, s1, s2, o0, o1, rd, wr, c=SM):
        op({"V": (f_ts(out, in0, s1, s2, o0, o1), c)}, rd, wr)

    def tt(out, a, b, o, rd, wr, c=SM):
        op({"V": (lambda: g.vector.tensor_tensor(out, a, b, o), c)}, rd, wr)

    def vcopy(out, a, rd, wr, c=SM):
        op({"V": (lambda: g.vector.tensor_copy(out, a), c)}, rd, wr)

    def copy(out, a, rd, wr, c):
        op({"V": (lambda: g.vector.tensor_copy(out, a), c), "S": (f_act(out, a, F.Copy), c)}, rd, wr)

    def shift(out, a, b, rd, wr, c):
        op({"V": (f_ts(out, a, b, None, A.add, None), c), "S": (f_act(out, a, F.Identity, bias=b), c)}, rd, wr)

    def fill(out, v, key, c=SM):
        op({"V": (lambda: g.vector.memset(out, v), c)}, [], [key])

    def act(out, a, fn, rd, wr, c=SM, **kw):
        op({"S": (f_act(out, a, fn, **kw), c)}, rd, wr)

    def mm(out, l, r, st, sp, rd, wr, c=PU):
        op({"P": (lambda: g.tensor.matmul(out, l, r, st, sp), c)}, rd, wr)

    def sums(bank, terms, st=True, sp=True):
        for j, (w, v) in enumerate(terms):
            mm(T[bank][:], T[w][:], T[v][:], st and j == 0, sp and j == len(terms) - 1, [w, v], [bank])

    def scan(out, data, add, init, rd, wr, c=SM):
        op({"V": (lambda: g.vector.tensor_tensor_scan(out, data, add, init, A.add, A.add), c)}, rd, wr)

    def total(out, a, rd, wr):
        op({"V": (lambda: g.vector.tensor_reduce(out, a, AX.X, A.add), SM)}, rd, wr)

    def iota(out, pat, base, cm, key, c, flag=True):
        if flag:
            op({"G": (lambda: g.iota(out, pat, base, cm, allow_small_or_imprecise_dtypes=True), c)}, [], [key])
        else:
            op({"G": (lambda: g.iota(out, pat, base, cm), c)}, [], [key])

    def many(n):
        return n * GU - (n - 1) * 0.06

    acol, rcol, pcol, wcol, ecol, mcol, ocol, lecol = [T.col[:, j:j + 1] for j in range(8)]
    mine = slice(16 * me, 16 * me + 16)

    dmas("Y", "lsz", [(T.szi[:], T.sz[:])], [], ["szi"])
    dmas("S", "lrf", [(T.rfi[:], T.rf[:])], [], ["rfi"])
    dmas("Y", "sth", [(T.sh[:, 0:32, :], T.rch[:]), (T.sh[:, 32:96, :], T.cd[:]), (T.sh[:, 96:128, :], T.rch[:])], [], ["sh"])
    dmas("S", "lco", [(T.cdo[:], T.cd[:])], [], ["cdo"])
    dmas("S", "lrg", [(T.rfj[:], T.rf[:])], [], ["rfj"])
    dmas("Y", "stown", [(T.dh[me, 32:96, :], T.cd[mine, :]), (T.dh[me, 0:32, :], T.rch[mine, :])], [], ["down"])
    iota(acol, [[1, 1]], -256, 1, "acol", 0.14)
    iota(T.nn[:], [[1, 512]], -256, 0, "nn", 1.2)
    iota(T.ai[:, 0:1], [[1, 1]], 0, 1, "ai0", 0.14, False)
    iota(T.cb[:], [[1, 8], [0, 16]], 0, 0, "cb", 0.4)
    iota(T.cp[:], [[0, 8], [1, 16]], 0, 0, "cp", 0.4)
    fill(T.zero[:], 0.0, "zero", U)
    fill(T.pre[:, 0:1], 0.0, "pre0")
    fill(T.one[:], 1.0, "one")
    ts(T.ib[:], T.nn[:, 0:128], acol, None, A.is_equal, None, ["nn", "acol"], ["ib"])
    ts(T.ih[:], T.nn[:, 0:128], acol, None, A.is_equal, None, ["nn", "acol"], ["ih"])
    send("rc", lambda r: T.sh[r], T.dh[me], ["sh"], "dh", PLAN["msg"])
    vcopy(T.szb[:], T.szi[:], ["szi"], ["szb"], U)
    for j in range(4):
        mm(T.pt0[:, j::4], T.szb[:, 128 * j:128 * j + 128], T.ib[:], True, True, ["szb", "ib"], ["pt0"], PU / 4)
    act(T.ln[:], T.szb[:], F.Copy, ["szb"], ["ln", "tot0"], U, accum_out=T.tot0[:, 0:1])
    ts(T.rfh[:], T.rfi[:], -2048.0, None, A.add, None, ["rfi"], ["rfh"], U)
    for j in range(4):
        mm(T.pt1[:, j::4], T.rfh[:, 128 * j:128 * j + 128], T.ih[:], True, True, ["rfh", "ih"], ["pt1"], PU / 4)
    act(T.ms[:, 0::2, 4], T.zero[:, 0:64], F.Identity, ["zero", "tot0"], ["mshi"], bias=T.tot0[:, 0:1])
    act(T.ms[:, :, 0:4], T.pt0[:], F.Copy, [], ["pt0", "ms"], U)
    ts(T.ms[:, 1::2, 4], T.ms[:, 0::2, 4], -1.0, T.tot0[:, 0:1], A.mult, A.add, ["mshi", "tot0"], ["mslo"])
    send("sz", lambda r: T.ms[:, 16 * r:16 * r + 16, :], T.ls[:, mine, :], ["ms", "mshi", "mslo"], "ls", PLAN["first"])
    vcopy(T.mr[:], T.pt1[:], [], ["pt1", "mr"], U)
    ts(T.ai[:, 1:2], T.ai[:, 0:1], 4, None, A.arith_shift_right, None, ["ai0"], ["ai1"])
    ts(T.ai[:, 2:3], T.ai[:, 0:1], 15, None, A.bitwise_and, None, ["ai0"], ["ai2"])
    vcopy(T.col[:, 1:3], T.ai[:, 1:3], ["ai1", "ai2"], ["rp"])
    ts(ecol, rcol, 17.0, pcol, A.mult, A.add, ["rp"], ["ecol"])
    ts(ecol, ecol, 8.0, 7.0 - 256.0, A.mult, A.add, [], ["ecol"])
    for c0, c1 in ((0, 512), (512, 1024), (1024, 1088)):
        ts(T.we[:, c0:c1], T.nn[:, 0:c1 - c0], float(c0), ecol, A.add, A.is_equal, ["nn", "ecol"], ["we%d" % c0], U / 2)
    for e in range(8):
        for u in range(8):
            c0 = 136 * e + 7 - u
            mm(T.pr[:, e::8], T.we[:, c0:c0 + 128], T.mr[:, :, 8 * u:8 * u + 8], u == 0, u == 7, ["we0", "we512", "we1024", "mr"], ["pr"], PU / 8)
    ts(T.lso[:], T.pr[:], 2048.0, None, A.add, None, [], ["pr", "lso"], U)
    send("rf", lambda r: T.lso[:, 64 * r:64 * r + 64], T.dl[me], ["lso"], "dl", PLAN["first"])
    dmas("Y", "lown", [(T.dl[me], T.lso[:, 64 * me:64 * me + 64])], ["lso"], ["dlown"])
    dmas("Y", "lst", [(T.lst[:], T.dl[:])], ["dl", "dlown"], ["lst"])
    act(T.ls[:, mine, :], T.ms[:, mine, :], F.Copy, ["ms", "mshi", "mslo"], ["lsown"])
    dmas("Y", "lrc", [(T.rchi[:], T.dh[:, 0:32, :])], ["dh", "down"], ["rchi"])
    dmas("Y", "lcd", [(T.cdi[:], T.dh[:, 32:96, :])], ["dh", "down"], ["cdi"])

    ts(T.blk512[:], T.cb[:], rcol, 512.0, A.is_equal, A.mult, ["cb", "rp"], ["blk512"], 0.16)
    vcopy(T.cdv[:], T.cdo[:], ["cdo"], ["cdv"])
    act(T.mm[:], T.nn[:, 0:512].indirect(T.cdv[:, 0:32]), F.Copy, ["nn", "cdv"], ["mm"], GU)
    tt(T.neq[:], T.rfi[:, 0:512].indirect(T.cdv[:, 0:32]), T.rfj[:], A.not_equal, ["rfi", "rfj", "cdv"], ["neq"], GU)
    sums("pt2", [("ib", "mm"), ("blk512", "neq")])
    tt(T.jc[:, 0:512], T.pt2[:], T.nn[:], A.min, ["nn"], ["pt2", "jc0"], U)
    shift(T.rko[:], T.rfh[:], 2048.0 - 255.5 + LIFT, ["rfh"], ["rko"], U)
    copy(T.rkp[:], T.rko[:], ["rko"], ["rkp"], U)
    tt(T.rl[:], T.rko[:, 0:512].indirect(T.cdv[:, 0:32]), T.rkp[:], A.not_equal, ["rko", "rkp", "cdv"], ["rl"], GU)
    sums("pt3", [("ib", "mm"), ("blk512", "rl")])
    ts(T.jc[:, 512:1024], T.pt3[:], 512.0, None, A.min, None, [], ["pt3", "jc1"], U)
    dmas("Y", "stc", [(T.sc[:], T.jc[0::16, :])], ["jc0", "jc1"], ["sc"])
    dmas("Y", "cown", [(T.dc[me], T.jc[16 * me:16 * me + 1, :])], ["jc0", "jc1"], ["dcown"])
    send("jc", lambda r: T.sc[r], T.dc[me], ["sc"], "dc", PLAN["msg"])

    fill(T.ll[:, 0:1], MID, "ll0")
    ts(T.ee[:], T.cp[:], pcol, None, A.is_equal, None, ["cp", "rp"], ["ee"], 0.16)
    ts(T.eq[:], T.nn[:, 0:8], 256.0, rcol, A.add, A.is_equal, ["nn", "rp"], ["eq"])
    ts(T.lt[:], T.nn[:, 0:8], 256.0, rcol, A.add, A.is_gt, ["nn", "rp"], ["lt"])
    for b in range(8):
        act(T.sel[:, 128 * b:128 * b + 128], T.ee[:], F.Identity, ["ee", "eq"], ["sel%d" % b], 0.16, scale=T.eq[:, b:b + 1])
    ts(wcol, rcol, 16.0, 15.0, A.mult, A.add, ["rp"], ["wcol"])
    ts(mcol, pcol, 0.0, None, A.is_equal, None, ["rp"], ["mcol"])
    ts(ocol, rcol, float(8 * me), -MID, A.add, A.mult, ["rp"], ["ocol"])
    tt(lecol, T.lt[:, me:me + 1], T.eq[:, me:me + 1], A.add, ["lt", "eq"], ["lecol"])
    ts(T.uu[:], T.lt[:], 16777216.0, None, A.mult, None, ["lt"], ["uu"])
    ts(T.wd[:], T.nn[:, 0:144], 256.0, wcol, A.add, A.is_equal, ["nn", "wcol"], ["wd"])
    tt(T.uu[:], T.uu[:], T.eq[:], A.add, ["eq"], ["uu"])
    for name, v in (("ni", -1.0), ("nk", -1024.0), ("ng", -2.0 ** 32), ("old", 2.0 ** 43), ("dgo", ocol)):
        ts(T[name][:], T.nn[:, 0:128], acol, v, A.is_equal, A.mult, ["nn", "acol", "ocol"], [name])
    ts(T.pb0[:], T.cb[:], rcol, mcol, A.is_equal, A.mult, ["cb", "rp", "mcol"], ["pb0"], 0.16)
    for name, v in (("pk", 1024.0), ("pg", 2.0 ** 32)):
        ts(T[name][:], T.pb0[:], v, None, A.mult, None, ["pb0"], [name])
    ts(T.blk16[:], T.cb[:], rcol, 16.0, A.is_equal, A.mult, ["cb", "rp"], ["blk16"], 0.16)
    ts(T.tmpc[:], T.cb[:], rcol, None, A.is_gt, None, ["cb", "rp"], ["tmpc"], 0.16)
    tt(T.e2[:], T.tmpc[:], T.ee[:], A.mult, ["tmpc", "ee"], ["e2"], 0.3)
    act(T.wb[:, 0:128], T.ee[:], F.Identity, ["ee", "lt"], ["wb0"], 0.16, scale=T.lt[:, me:me + 1])
    act(T.wb[:, 128:256], T.ee[:], F.Identity, ["ee", "lecol"], ["wb1"], 0.16, scale=lecol)
    MW = ["mw%d" % b for b in range(8)]
    for o, key in [(T.mwin[:, 512 * b:512 * b + 512], MW[b]) for b in range(8)] + [(T[k][:], k) for k in ("cc", "j1", "jn")]:
        op({"V": (f_ts(o, T.nn[:], 0.0, None, A.mult, None), U / 2), "S": (f_act(o, T.zero[:], F.Copy), U)}, ["nn", "zero"], [key])
    later[0] = 100
    vcopy(T.rchf[:], T.rchi[:], ["rchi"], ["rchf"])
    ts(T.scl[:], T.rchi[:], 0.5, None, A.add, None, ["rchi"], ["scl"])
    op({"V": (lambda: g.vector.reciprocal(T.rec[:], T.scl[:]), 0.3)}, ["scl"], ["rec"])
    ts(T.rec[:], T.rec[:], TURN, None, A.mult, None, [], ["rec"])
    ts(T.steps[:], T.nn[:, 0:16], 248.0, 2.0 ** -24, A.add, A.mult, ["nn"], ["steps"])
    for k in range(16):
        c0 = T.rec[:, k:k + 1]
        act(T.cand[:, k, :], T.steps[:], F.Identity, ["steps", "rec"], ["cand%d" % k], scale=c0, bias=c0)
    for k in range(16):
        act(T.fits[:, k, :], T.cand[:, k, :], F.Abs, ["cand%d" % k, "rchf"], ["fits%d" % k], scale=T.rchf[:, k:k + 1])
    ts(T.fits[:], T.fits[:], TURN, None, A.is_le, None, ["fits%d" % k for k in range(16)], ["fits"], U / 2)
    tt(T.cand[:], T.cand[:], T.fits[:], A.mult, ["fits"], ["cand%d" % k for k in range(16)] + ["cand"], U)
    for w in (8, 4, 2):
        tt(T.cand[:, :, 0:w], T.cand[:, :, 0:w], T.cand[:, :, w:2 * w], A.max, [], ["cand"], U * w / 16)
    tt(T.scl[:], T.cand[:, :, 0], T.cand[:, :, 1], A.max, ["cand"], ["scl"])
    vcopy(T.cdu[:], T.cdi[:], ["cdi"], ["cdu"])
    later[0] = 0

    BW = ["bw%d" % b for b in range(8)]

    def table(banks):
        def part(b, j):
            mm(T[banks[b]][:], T.sel[:, 128 * b:128 * b + 128], T[("hc", "lc")[j]][:], j == 0, j == 1, ["sel%d" % b, ("hc", "lc")[j]], [banks[b]])
        for j in range(2):
            for b in range(8):
                if banks[b] not in banks[:b]:
                    part(b, j)
        for b in range(8):
            shift(T.bwin[:, 512 * b:512 * b + 512], T[banks[b]][:], T.bias[:, b:b + 1], ["bias"], [banks[b], BW[b]], U)
            for again in range(b + 1, 8):
                if banks[again] == banks[b]:
                    part(again, 0)
                    part(again, 1)

    for bank in ("pm", "pr"):
        for j in range(4):
            mm(T[bank][:, 128 * j:128 * j + 128], T.ls[:, :, j], T.ib[:], True, True, ["ls", "lsown", "ib"], [bank], PU / 4)
    act(T.szr[:], T.pm[:], F.Copy, [], ["pm", "szr"], U)
    tt(T.x8[:], T.ls[:, 0::16, 4], T.ls[:, 1::16, 4], A.add, ["ls", "lsown"], ["x8"])
    scan(T.pre[:, 1:9], T.x8[:], T.zero[:, 0:8], 0.0, ["x8", "zero"], ["pre"])
    ts(T.z8[:], T.x8[:], T.lt[:, me:me + 1], None, A.mult, None, ["x8", "lt"], ["z8"])
    mm(T.pn[:, 0:8], T.ee[:], T.pre[:, 0:8], True, False, ["ee", "pre", "pre0"], ["pn"], PU / 2)
    mm(T.pn[:, 0:8], T.ee[:], T.z8[:], False, True, ["ee", "z8"], ["pn"], PU / 2)
    scan(T.ll[:, 1:512], T.pr[:, 0:511], T.zero[:, 0:511], MID, ["zero"], ["pr", "ll"], U)
    tt(T.x8[:], T.pn[:, 0:8], T.eq[:], A.mult, ["eq"], ["pn", "x8"])
    total(T.own[:, 0:1], T.x8[:], ["x8"], ["own"])
    ts(T.bias[:], T.pn[:, 0:8], T.own[:, 0:1], MID, A.subtract, A.add, ["own"], ["pn", "bias"])
    act(T.bwin[:, 0::512], T.bias[:], F.Copy, ["bias"], ["bw"])
    for b, bank in enumerate(["pf", "pt0", "pt1", "pt2", "pt3", "pm", "pf", "pt0"]):
        mm(T[bank][:], T.sel[:, 128 * b:128 * b + 128], T.szr[:], True, True, ["sel%d" % b, "szr"], [bank])
        scan(T.bwin[:, 512 * b + 1:512 * b + 512], T[bank][:, 0:511], T.zero[:, 0:511], T.bias[:, b:b + 1], ["zero", "bias"], [bank, BW[b]], U)

    def folds(t):
        if t == 1:
            m = "j1"
            dmas("Y", "mw1", [(T.mwin[16 * r:16 * r + 1, :], T.dc[:, 0:64, :]) for r in range(8)], ["dc", "dcown"], MW)
            dmas("Y", "lj1", [(T.j1[0::16, :], T.dc[:, 0:64, :])], ["dc", "dcown"], ["j1"])
            dmas("Y", "lcc", [(T.cc[0::16, :], T.dc[:, 64:128, :])], ["dc", "dcown"], ["cc"])
        else:
            m = "mm"
            if PLAN["neq"] == "V":
                tt(T.neq[:], T.rl[:, 0:512].indirect(T.cdu[:, 0:32]), T.rl2[:], A.not_equal, ["rl", "rl2", "cdu"], ["neq"], GU)
            else:
                act(T.rl2[:], T.rl[:, 0:512].indirect(T.cdu[:, 0:32]), F.Copy, ["rl", "cdu"], ["rl2"], GU)
                sums("pr", [("ni", "rl"), ("ib", "rl2")])
                act(T.neq[:], T.pr[:], F.Abs, [], ["pr", "neq"], U)
            sums("pr", [("pb0", "cc"), ("blk512", "neq")])
            tt(T.jj[:], T.pr[:], T.nn[:], A.min, ["nn"], ["pr", "jj"], U)
            if t < RO:
                copy(T.mm[:], T.jj[:, 0:512].indirect(T.ml[:, 32 * (t - 2):32 * (t - 1)]), ["jj", "ml%d" % t], ["mm"], GU)
                dmas("Y", "mw%d" % t, [(T.mwin[0::16, 512 * p:512 * p + 512], T.mm[16 * p:16 * p + 8, :]) for p in range(8)], ["mm"], MW)
        if t < RO:
            for p in range(16):
                mm(T.pr[:, 0:32], T.wd[:, 15 - p:143 - p], T[m][:, p::16], p == 0, p == 15, ["wd", m], ["pr"], PU / 8)
            ts(T.ml[:, 32 * (t - 1):32 * t], T.pr[:, 0:32], 1.0 if t == 1 else 0.0625, 256.0, A.mult, A.add, [], ["pr", "ml%d" % (t + 1)])

    def home():
        dmas("Y", "str", [(T.sr[:], T.rl[:])], ["rl"], ["sr"])
        dmas("Y", "rown", [(T.dr[me], T.rl[mine, :])], ["rl"], ["drown"])
        dmas("Y", "stj", [(T.sj[:], T.jj[0::16, :])], ["jj"], ["sj"])
        dmas("Y", "jown", [(T.dj[me], T.jj[16 * me:16 * me + 1, :])], ["jj"], ["djown"])
        send("ro", lambda r: T.sr[r], T.dr[me], ["sr", "tot3"], "dr", PLAN["big"])
        send("jo", lambda r: T.sj[r], T.dj[me], ["sj"], "dj", PLAN["msg"])
        dmas("Y", "ljn", [(T.jn[0::16, :], T.dj[:])], ["dj", "djown"], ["jn"])
        dmas("Y", "lj8", [(T.j8[0:8, :], T.dj[:])], ["dj", "djown"], ["j8"])
        dmas("Y", "lrn", [(T.rn[:], T.dr[:])], ["dr", "drown"], ["rn"])
        for j in range(4):
            mm(T.pt1[:, j::4], T.jj[:, 128 * j:128 * j + 128], T.ib[:], True, False, ["jj", "ib"], ["pt1"], PU / 4)
            mm(T.pt1[:, j::4], T.nn[:, 128 * j:128 * j + 128], T.ni[:], False, True, ["nn", "ni"], ["pt1"], PU / 4)
        ts(T.alv[:], T.pt1[:], 0.0, 1.0, A.is_equal, A.add, [], ["pt1", "alv"], U)

    def renames(t):
        k = 0
        for n in RENAMES:
            copy(T.gr[:, 512 * k:512 * (k + n)], T.mwin[:, 0:4096].indirect(T.lst[:, 32 * k:32 * (k + n)]), MW + ["lst"],
                 ["gr%d" % (k + j) for j in range(n)], many(n))
            k += n
        for name, out in (("r", "rl"), ("q", "rl2"))[:2 if PLAN["neq"] == "V" else 1]:
            dmas("Y", name + str(t), [(T[out][:], T.gr[0::16, :])], ["gr%d" % j for j in range(16)], [out])

    def marks(t):
        def over(k):
            o = T.ind[:, 512 * k:512 * k + 512]
            i = op({"V": (f_ts(o, o, EDGE, None, A.is_gt, None), U / 2 + 0.03), "S": (f_act(o, o, F.Relu, bias=-EDGE), U)}, [], ["ind%d" % k])
            calls[i]["first"] = OVER[t - 1][k]
            mm(T.pf[:], T.wd[:, 15 - k:143 - k], o, k == 0 and t == 1, k == 15, ["wd", "ind%d" % k], ["pf"])

        dmas("Y", "l%d" % t, [(T.ll[:, 512:1024], T.ll[:, 0:512])], ["ll", "ll0"], ["l2"])
        k = 0
        for n in GATHERS:
            tt(T.dd[:, 512 * k:512 * (k + n)], T.bwin[:, 0:4096].indirect(T.lst[:, 32 * k:32 * (k + n)]), T.ll[:, 0:512 * n], A.subtract,
               BW + ["bw", "lst", "ll", "ll0"] + ["l2"] * (n - 1), ["dd%d" % (k + j) for j in range(n)], many(n))
            for j in range(k, k + n):
                act(T.ind[:, 512 * j:512 * j + 512], T.dd[:, 512 * j:512 * j + 512], F.Abs, ["dd%d" % j, "scl"], ["ind%d" % j], U, scale=T.scl[:, j:j + 1])
                if j >= PLAN["lag"]:
                    over(j - PLAN["lag"])
            k += n
        for j in range(16 - PLAN["lag"], 16):
            over(j)

    folds(1)
    for t in range(1, RO + 1):
        if t > 1:
            sums("pf", [("pg", "j1" if t == 2 else "jj"), ("ng", "nn"), ("old", "far")], sp=False)
            renames(t)
            folds(t)
        if t == RO:
            home()
        marks(t)
        sums("pm", [("pk", "j1" if t == 1 else "jj"), ("nk", "nn"), ("ib", "szr")], sp=False)
        ts(T.far[:], T.pf[:], 0.0, None, A.is_gt, None, [], ["pf", "far"], U)
        tcol = T.tot[:, (8 * (t - 1) + me) * 4:(8 * (t - 1) + me) * 4 + 1] if t < RO else T.tot0[:, 4:5]
        sums("pm", [("blk16", "far")], st=False)
        act(T.ln[:], T.pm[:], F.Relu, [], ["pm", "ln", "totown"], U, accum_out=tcol)
        if t == RO:
            break
        lists_t = T.ml[:, 32 * (t - 1):32 * t]
        send("t%d" % t, lambda r: tcol, tcol, ["totown"], "tot%d" % t, PLAN["msg"])
        scan(T.ll[:, 1:512], T.ln[:, 0:511], T.zero[:, 0:511], MID, ["ln", "zero"], ["ll"], U)
        copy(T.hc[:], T.ll[:, 0:512].indirect(lists_t), ["ll", "ll0", "ml%d" % (t + 1)], ["hc"], GU)
        tt(T.lc[:], T.ll[:, 0:512].indirect(lists_t), T.hc[:], A.subtract, ["ll", "ll0", "hc", "ml%d" % (t + 1)], ["lc"], GU)
        scan(T.pre[:, 1:9], T.tot[:, 32 * (t - 1):32 * t:4], T.zero[:, 0:8], 0.0, ["tot%d" % t, "totown", "zero"], ["pre"])
        mm(T.pn[:, 8:9], T.e2[:], T.pre[:, 8:9], True, True, ["e2", "pre"], ["pn"], PU / 2)
        if me == 0:
            ts(T.z8[:], T.lt[:], T.pre[:, 8:9], None, A.mult, None, ["uu", "pre"], ["z8"])
        else:
            ts(T.z8[:], T.uu[:], T.pre[:, me:me + 1], T.pre[:, 8:9], A.mult, A.min, ["uu", "pre"], ["z8"])
        mm(T.pn[:, 0:8], T.ee[:], T.z8[:], True, True, ["ee", "z8"], ["pn"], PU / 2)
        ts(T.bias[:], T.pn[:, 0:8], T.pn[:, 8:9], T.pre[:, me:me + 1], A.subtract, A.subtract, ["pre", "pre0"], ["pn", "bias"])
        table(["pf", "pt0", "pt1", "pt2", "pt3", "pm", "pf", "pt0"])

    for j in range(4):
        mm(T.pt0[:, j::4], T.far[:, 128 * j:128 * j + 128], T.ib[:], True, True, ["far", "ib"], ["pt0"], PU / 4)
    tt(T.ft[:, :, 0:4], T.pt0[:], T.alv[:], A.mult, ["alv"], ["pt0", "ft"], U)
    ts(T.ft[:, 0::2, 4], T.zero[:, 0:64], tcol, MID, A.add, A.add, ["zero", "totown"], ["fthi"])
    ts(T.own[:, 2:3], tcol, MID, None, A.add, None, ["totown"], ["own2"])
    ts(T.ft[:, 1::2, 4], T.ft[:, 0::2, 4], -1.0, T.own[:, 2:3], A.mult, A.add, ["fthi", "own2"], ["ftlo"])
    send("fo", lambda r: T.ft[:, 16 * r:16 * r + 16, :], T.lf[:, mine, :], ["ft", "fthi", "ftlo"], "lf", PLAN["msg"] + 1.0)
    vcopy(T.lf[:, mine, :], T.ft[:, mine, :], ["ft", "fthi", "ftlo"], ["lfown"])
    sums("pr", [("ib", "rko"), ("ib", "rn")])
    shift(T.rr[:], T.pr[:], 256.0 - LIFT, [], ["pr", "rr"], U)
    dmas("Y", "yr", [(T.yr[:], T.rr[:])], ["rr"], [])
    sums("pr", [("pk", "jn"), ("nk", "nn"), ("ib", "szb")])
    act(T.sza[:], T.pr[:], F.Relu, [], ["pr", "sza"], U)
    shift(T.j8f[0:8, :], T.j8[0:8, :], float(256 + S * me), ["j8"], ["j8f"], U)
    dmas("Y", "yj", [(T.yj[:], T.j8f[0:8, :])], ["j8f"], [])
    sums("pt3", [("ib", "sza")], sp=False)
    mm(T.pn[:, 0:1], T.dgo[:], T.one[:, 0:1], True, False, ["dgo", "one"], ["pn"], PU / 8)
    for j in range(4):
        mm(T.pt1[:, 128 * j:128 * j + 128], T.lf[:, :, j], T.ib[:], True, True, ["lf", "lfown", "ib"], ["pt1"], PU / 4)
    act(T.farn[:], T.pt1[:], F.Relu, [], ["pt1", "farn"], U, bias=-1.0)
    for b in range(16):
        c0 = 112 - 16 * (b // 2)
        mm(T.pn[:, 0:1], T.wb[:, c0:c0 + 128], T.lf[:, 16 * (b // 2) + b % 2, 4:5], False, b == 15, ["wb0", "wb1", "lf", "lfown"], ["pn"], PU / 8)
    sums("pt3", [("blk16", "farn")], st=False)
    for j in range(4):
        mm(T.pt2[:, 128 * j:128 * j + 128], T.lf[:, :, j], T.ib[:], True, True, ["lf", "lfown", "ib"], ["pt2"], PU / 4)
    vcopy(T.la[:, 0:1], T.pn[:, 0:1], [], ["pn", "la0"])
    scan(T.la[:, 1:512], T.pt3[:, 0:511], T.zero[:, 0:511], T.la[:, 0:1], ["la0", "zero"], ["pt3", "la"], U)
    dmas("Y", "ya", [(T.ya[:], T.la[:, 0:512])], ["la", "la0"], [])
    act(T.yfb[:], T.pt2[:], F.Sign, [], ["pt2", "yfb"], U)
    dmas("S", "yf", [(T.yf[:], T.yfb[:])], ["yfb"], [])

    count = {"V": 0, "S": 0, "P": 0, "G": 0}
    seen = {q: {} for q in Q}
    token, most = {}, {}
    if not ORDER:
        ORDER.extend(place(calls))
    for i, q in ORDER:
        c = calls[i]
        if q != "-":
            want = {}
            for d in c["deps"]:
                s, v = token[d]
                if (s == "P" and q == "P") or (q == "G" and s.startswith("o_")):
                    continue
                want[s] = max(want.get(s, 0), v)
            for s, v in want.items():
                if seen[q].get(s, 0) < v:
                    Q[q].wait_ge(T.sem[s], v)
                    seen[q][s] = v
            made = c["alts"][q][0]()
            if c["tok"] is None:
                count[q] += 1
                made.then_inc(T.sem[q], 1)
        token[i] = c["tok"] or (q, count[q])
        most[token[i][0]] = max(most.get(token[i][0], 0), token[i][1])
    for s, v in most.items():
        if max(seen[q].get(s, 0) for q in seen) < v:
            g.wait_ge(T.sem[s], v)
